import numpy as np
import ml_dtypes


def mxq(x, axis, fmt="e4m3"):
    dtype, down = {"e4m3": (ml_dtypes.float8_e4m3fn, 7), "e5m2": (ml_dtypes.float8_e5m2, 14)}[fmt]
    v = np.moveaxis(np.asarray(x, np.float32).astype(ml_dtypes.bfloat16).astype(np.float64), axis, -1)
    blocks = v.reshape(v.shape[:-1] + (-1, 32))
    amax = np.abs(blocks).max(-1, keepdims=True)
    byte = np.maximum(np.where(amax > 0, np.frexp(amax)[1] - 1 + 127, 0) - down, 1)
    scale = np.exp2(byte - 127.0)
    codes = (blocks / scale).astype(np.float32).astype(dtype).astype(np.float64)
    return np.moveaxis((codes * scale).reshape(v.shape), -1, axis)


WIDE = False


def mx_kscale(k):
    if not WIDE:
        return np.ones(k)
    levels = np.array([10, -10, 5, -5, 0])
    if k % 512:
        return np.exp2(np.random.permutation(np.resize(levels, k // 32))).repeat(32)
    a = np.empty((k // 512, 16))
    for p in range(k // 512):
        a[p, :8] = np.random.permutation(np.resize(levels, 8))
        for g in range(8):
            far = levels[np.abs(levels - a[p, g]) >= 10]
            a[p, g + 8] = far[np.random.randint(len(far))]
    return np.exp2(a.ravel()).repeat(32)


def f64(x):
    return np.asarray(x).astype(np.float64)


def striped(idx):
    return np.tile(idx.reshape(-1, 16).T, (8, 1)).astype(np.uint16)


def unstriped(offs):
    return offs[:16].T.reshape(-1).astype(np.int64)


E2M1 = np.array([0.0, 0.5, 1.0, 1.5, 2.0, 3.0, 4.0, 6.0, -0.0, -0.5, -1.0, -1.5, -2.0, -3.0, -4.0, -6.0])


def pack_fp4(w):
    k, n = w.shape
    w = f64(np.asarray(w, np.float32).astype(ml_dtypes.bfloat16)).reshape(k // 32, 32, n)
    amax = np.abs(w).max(1)
    mant, ex = np.frexp(amax / 6.0)
    byte = np.clip(np.where(amax > 0, np.where(mant > 0.5, ex, ex - 1) + 127, 1), 1, 254)
    scaled = (w * np.exp2(127.0 - byte)[:, None, :]).reshape(k, n).astype(np.float32)
    c = np.ascontiguousarray(scaled.reshape(k // 512, 128, 4, n).transpose(0, 1, 3, 2)).astype(ml_dtypes.float4_e2m1fn).view(np.uint8) & 0xF
    words = (c[..., 0::2] | (c[..., 1::2] << 4)).reshape(k // 512, 128, 2 * n)
    return np.ascontiguousarray(words), np.ascontiguousarray(byte.astype(np.uint8).reshape(k // 512, 16, n))


def unpack_fp4(words, scales):
    g, _, n = scales.shape
    words = np.ascontiguousarray(words).reshape(g, 128, n, 2)
    nib = np.empty((g, 128, n, 4), np.uint8)
    nib[..., 0::2] = words & 0xF
    nib[..., 1::2] = words >> 4
    vals = E2M1[nib] * np.repeat(np.exp2(scales.astype(np.float64) - 127.0), 8, axis=1)[..., None]
    return vals.transpose(0, 1, 3, 2).reshape(g * 512, n)


def relu(v):
    return np.maximum(v, 0.0)


K, T, S, H, N, U = 512, 1024, 512, 512, 128, 1024
P = 2 ** 7


def setup_inputs():
    n = np.random.standard_normal
    s = mx_kscale(K)[:, None]
    u = mx_kscale(H)
    packed_w2 = pack_fp4(n((H, N)) / np.sqrt(H) / u[:, None])
    return {
        "xT": (n((K, T)) * s).astype(np.float32),
        "gate": np.tile(np.random.uniform(0.5, 1.5, S), (P, 1)).astype(np.float32),
        "w1": (n((K, H)) / np.sqrt(K) / s * u).astype(np.float32),
        "w2_words": packed_w2[0],
        "w2_scales": packed_w2[1],
        "offs": striped(np.random.permutation(T)[:S]),
        "dst": striped(np.random.permutation(U)[:S]),
    }


def reference(xT, gate, w1, w2_words, w2_scales, offs, dst):
    xq = mxq(f64(xT)[:, unstriped(offs)], 0, "e4m3")
    h = relu(mxq(f64(w1), 0, "e4m3").T @ xq)
    y = unpack_fp4(w2_words, w2_scales).T @ mxq(h, 0, "e4m3")
    out = np.zeros((N, U))
    out[:, unstriped(dst)] = y * f64(gate)[:1]
    return out

@@ -1,0 +1,157 @@
+from contextlib import ExitStack
+
+import concourse.mybir as mybir
+
+K, T, S, H, N, U = 512, 1024, 512, 512, 128, 1024
+FLOPS = 2 * K * H * S + 2 * H * N * S
+
+F32 = mybir.dt.float32
+BF16 = mybir.dt.bfloat16
+I32 = mybir.dt.int32
+U32 = mybir.dt.uint32
+U16 = mybir.dt.uint16
+U8 = mybir.dt.uint8
+FP8X4 = mybir.dt.float8_e4m3fn_x4
+FP4X4 = mybir.dt.float4_e2m1fn_x4
+COPY = mybir.ActivationFunctionType.Copy
+RELU = mybir.ActivationFunctionType.Relu
+MULT = mybir.AluOpType.mult
+
+P = 128
+PACK = 4
+X_PIECES = [256,256,256,256]
+X_SCALAR = [96,96,96,96]
+W_PIECES = [128,128,128,128]
+W_SCALAR = [128,128,128,0]
+CH = 128
+
+
+def tile_picked_route2_mlprelu_e_kernel(tc, xT, gate, w1, w2_words, w2_scales, offs, dst, out):
+    nc = tc.nc
+    with ExitStack() as ctx:
+        keep = ctx.enter_context(tc.tile_pool(name="keep", bufs=1))
+        psum = ctx.enter_context(tc.psum_pool(name="psum", bufs=1))
+
+        offs_t = keep.tile([P, S // 16], U16, name="offs_t")
+        dst_t = keep.tile([P, S // 16], U16, name="dst_t")
+        x_words = keep.tile([P, T], U32, name="x_words", align_bytes=64)
+        x_bytes = keep.tile([P, T], U8, name="x_bytes", align_bytes=64)
+        w2_codes = keep.tile([P, 2 * N], U8, name="w2_codes", align_bytes=64)
+        w2_plane = keep.tile([P, N], U8, name="w2_plane", align_bytes=64)
+        gate_t = keep.tile([P, S], F32, name="gate_t")
+        window = keep.tile([P, U], F32, name="window")
+
+        nc.vector.memset(w2_plane[:].bitcast(I32), 0)
+        nc.vector.memset(x_bytes[:].bitcast(I32), 0)
+        nc.vector.memset(window[:], 0.0)
+
+        nc.sync.dma_start(offs_t[:], offs)
+        x_view = xT.rearrange("(p j) t -> p j t", j=PACK)
+        x_raw = []
+        c0 = 0
+        for i, w in enumerate(X_PIECES):
+            raw = keep.tile([P, PACK, w], F32, name="x_raw%d" % i)
+            nc.sync.dma_start(raw[:], x_view[:, :, c0:c0 + w])
+            x_raw.append(raw)
+            c0 = c0 + w
+        w_view = w1.rearrange("(p j) c -> p j c", j=PACK)
+        w_raw = []
+        c0 = 0
+        for i, w in enumerate(W_PIECES):
+            raw = keep.tile([P, PACK, w], F32, name="w_raw%d" % i)
+            nc.sync.dma_start(raw[:], w_view[:, :, c0:c0 + w])
+            w_raw.append(raw)
+            c0 = c0 + w
+        nc.sync.dma_start(w2_codes[:].bitcast(I32), w2_words[0].bitcast(I32))
+        for q in range(4):
+            nc.sync.dma_start(w2_plane[32 * q:32 * q + 4, :].bitcast(I32), w2_scales[0, 4 * q:4 * q + 4, :].bitcast(I32))
+        nc.sync.dma_start(dst_t[:], dst)
+        nc.sync.dma_start(gate_t[:], gate)
+
+        c0 = 0
+        for i, w in enumerate(X_PIECES):
+            grouped = keep.tile([P, w, PACK], BF16, name="x_grouped%d" % i, align_bytes=64)
+            s = X_SCALAR[i]
+            if s > 0:
+                nc.scalar.activation(grouped[:, 0:s, :].rearrange("p (c i) j -> p c j i", i=4),
+                                     x_raw[i][:, :, 0:s].rearrange("p j (c i) -> p c j i", i=4), COPY)
+            if s < w:
+                nc.vector.tensor_copy(grouped[:, s:w, :].rearrange("p (c i) j -> p c j i", i=4),
+                                      x_raw[i][:, :, s:w].rearrange("p j (c i) -> p c j i", i=4))
+            nc.vector.quantize_mx(out=x_words[:, c0:c0 + w].bitcast(FP8X4), scales=x_bytes[:, c0:c0 + w],
+                                  in_=grouped[:].rearrange("p c j -> p (c j)"))
+            c0 = c0 + w
+
+        g_words, g_bytes = [], []
+
+        def gather(c):
+            gw = keep.tile([P, CH], U32, name="g_words%d" % c, align_bytes=64)
+            gb = keep.tile([P, CH], U8, name="g_bytes%d" % c, align_bytes=64)
+            sl = offs_t[:, c * CH // 16:(c + 1) * CH // 16]
+            nc.vector.tensor_copy(gw[:], x_words[:].indirect(sl))
+            nc.vector.tensor_copy(gb[:], x_bytes[:].indirect(sl))
+            g_words.append(gw)
+            g_bytes.append(gb)
+
+        for c in range(2):
+            gather(c)
+
+        w_grouped = keep.tile([P, PACK, P, PACK], BF16, name="w_grouped", align_bytes=64)
+        c0 = 0
+        for i, w in enumerate(W_PIECES):
+            s = W_SCALAR[i]
+            if s > 0:
+                nc.scalar.activation(w_grouped[:, :, c0 // 4:(c0 + s) // 4, :].rearrange("p t m j -> p m j t"),
+                                     w_raw[i][:, :, 0:s].rearrange("p j (m t) -> p m j t", t=4), COPY)
+            if s < w:
+                nc.vector.tensor_copy(w_grouped[:, :, (c0 + s) // 4:(c0 + w) // 4, :].rearrange("p t m j -> p m j t"),
+                                      w_raw[i][:, :, s:w].rearrange("p j (m t) -> p m j t", t=4))
+            c0 = c0 + w
+        w_words, w_bytes = [], []
+        for t in range(PACK):
+            ww = keep.tile([P, P], U32, name="w_words%d" % t, align_bytes=64)
+            wb = keep.tile([P, P], U8, name="w_bytes%d" % t, align_bytes=64)
+            nc.vector.quantize_mx(out=ww[:].bitcast(FP8X4), scales=wb[:],
+                                  in_=w_grouped[:, t, :, :].rearrange("p m j -> p (m j)"))
+            w_words.append(ww)
+            w_bytes.append(wb)
+
+        for c in range(2, S // CH):
+            gather(c)
+
+        def layer1(c):
+            acc = psum.tile([P, PACK, CH], F32, name="h_acc%d" % c)
+            for t in range(PACK):
+                nc.tensor.matmul_mx(out=acc[:, t, :], lhsT=w_words[t][:].bitcast(FP8X4), lhsT_scale=w_bytes[t][:],
+                                    rhs=g_words[c][:].bitcast(FP8X4), rhs_scale=g_bytes[c][:], start=True, stop=True)
+            hg = keep.tile([P, CH, PACK], BF16, name="h_grouped%d" % c, align_bytes=64)
+            nc.scalar.activation(hg[:], acc[:].rearrange("p t n -> p n t"), RELU)
+            return hg
+
+        def layer2(c, hg):
+            hw = keep.tile([P, CH], U32, name="h_words%d" % c, align_bytes=64)
+            hb = keep.tile([P, CH], U8, name="h_bytes%d" % c, align_bytes=64)
+            nc.vector.quantize_mx(out=hw[:].bitcast(FP8X4), scales=hb[:], in_=hg[:].rearrange("p n t -> p (n t)"))
+            acc = psum.tile([P, CH], F32, name="y_acc%d" % c)
+            nc.tensor.matmul_mx(out=acc[:], lhsT=w2_codes[:].bitcast(FP4X4), lhsT_scale=w2_plane[:],
+                                rhs=hw[:].bitcast(FP8X4), rhs_scale=hb[:], start=True, stop=True)
+            y = keep.tile([P, CH], F32, name="y%d" % c)
+            nc.scalar.activation(y[:], acc[:], COPY)
+            return y
+
+        def scatter(c, y):
+            nc.vector.tensor_tensor(window[:].indirect(dst_t[:, c * CH // 16:(c + 1) * CH // 16]), y[:],
+                                    gate_t[:, c * CH:(c + 1) * CH], MULT)
+
+        n = S // CH
+        hs, ys = {}, {}
+        for step in range(n + 2):
+            if step < n:
+                hs[step] = layer1(step)
+            if 1 <= step <= n:
+                ys[step - 1] = layer2(step - 1, hs[step - 1])
+            if step >= 2:
+                scatter(step - 2, ys[step - 2])
+
+        nc.sync.dma_start(out[:, 0:U // 2], window[:, 0:U // 2])
+        nc.scalar.dma_start(out[:, U // 2:U], window[:, U // 2:U])

@@ -19,17 +19,20 @@ MULT = mybir.AluOpType.mult
 
 P = 128
 PACK = 4
-X_PIECES = [256,256,256,256]
-X_SCALAR = [96,96,96,96]
+X_PIECES = [256,256,256,128,128]
+X_SCALAR = [96,96,96,48,48]
 W_PIECES = [128,128,128,128]
-W_SCALAR = [128,128,128,0]
+W_SCALAR = [128,128,128,48]
 CH = 128
+H_BANK = ["a","b","c","b"]
+Y_BANK = ["e","f","g","h"]
 
 
 def tile_picked_route2_mlprelu_e_kernel(tc, xT, gate, w1, w2_words, w2_scales, offs, dst, out):
     nc = tc.nc
     with ExitStack() as ctx:
         keep = ctx.enter_context(tc.tile_pool(name="keep", bufs=1))
+        late = ctx.enter_context(tc.tile_pool(name="late", bufs=1))
         psum = ctx.enter_context(tc.psum_pool(name="psum", bufs=1))
 
         offs_t = keep.tile([P, S // 16], U16, name="offs_t")
@@ -41,31 +44,30 @@ def tile_picked_route2_mlprelu_e_kernel(tc, xT, gate, w1, w2_words, w2_scales, o
         gate_t = keep.tile([P, S], F32, name="gate_t")
         window = keep.tile([P, U], F32, name="window")
 
-        nc.vector.memset(w2_plane[:].bitcast(I32), 0)
         nc.vector.memset(x_bytes[:].bitcast(I32), 0)
         nc.vector.memset(window[:], 0.0)
 
-        nc.sync.dma_start(offs_t[:], offs)
         x_view = xT.rearrange("(p j) t -> p j t", j=PACK)
-        x_raw = []
-        c0 = 0
-        for i, w in enumerate(X_PIECES):
-            raw = keep.tile([P, PACK, w], F32, name="x_raw%d" % i)
-            nc.sync.dma_start(raw[:], x_view[:, :, c0:c0 + w])
-            x_raw.append(raw)
-            c0 = c0 + w
         w_view = w1.rearrange("(p j) c -> p j c", j=PACK)
-        w_raw = []
-        c0 = 0
-        for i, w in enumerate(W_PIECES):
-            raw = keep.tile([P, PACK, w], F32, name="w_raw%d" % i)
-            nc.sync.dma_start(raw[:], w_view[:, :, c0:c0 + w])
-            w_raw.append(raw)
-            c0 = c0 + w
+        x_raw = [keep.tile([P, PACK, w], F32, name="x_raw%d" % i) for i, w in enumerate(X_PIECES)]
+        w_raw = [keep.tile([P, PACK, w], F32, name="w_raw%d" % i) for i, w in enumerate(W_PIECES[:-1])]
+        w_raw.append(late.tile([P, PACK, W_PIECES[-1]], F32, name="w_raw_last", offset=4096, align_bytes=64))
+        nc.sync.dma_start(x_raw[0][:], x_view[:, :, sum(X_PIECES[:0]):sum(X_PIECES[:1])])
+        nc.sync.dma_start(w2_plane[0:4, :].bitcast(I32), w2_scales[0, 0:4, :].bitcast(I32))
+        nc.sync.dma_start(w2_plane[32:36, :].bitcast(I32), w2_scales[0, 4:8, :].bitcast(I32))
+        nc.sync.dma_start(w2_plane[64:68, :].bitcast(I32), w2_scales[0, 8:12, :].bitcast(I32))
+        nc.sync.dma_start(w2_plane[96:100, :].bitcast(I32), w2_scales[0, 12:16, :].bitcast(I32))
+        nc.sync.dma_start(offs_t[:], offs)
+        nc.sync.dma_start(x_raw[1][:], x_view[:, :, sum(X_PIECES[:1]):sum(X_PIECES[:2])])
+        nc.sync.dma_start(x_raw[2][:], x_view[:, :, sum(X_PIECES[:2]):sum(X_PIECES[:3])])
+        nc.sync.dma_start(x_raw[3][:], x_view[:, :, sum(X_PIECES[:3]):sum(X_PIECES[:4])])
+        nc.sync.dma_start(x_raw[4][:], x_view[:, :, sum(X_PIECES[:4]):sum(X_PIECES[:5])])
         nc.sync.dma_start(w2_codes[:].bitcast(I32), w2_words[0].bitcast(I32))
-        for q in range(4):
-            nc.sync.dma_start(w2_plane[32 * q:32 * q + 4, :].bitcast(I32), w2_scales[0, 4 * q:4 * q + 4, :].bitcast(I32))
         nc.sync.dma_start(dst_t[:], dst)
+        nc.sync.dma_start(w_raw[0][:], w_view[:, :, sum(W_PIECES[:0]):sum(W_PIECES[:1])])
+        nc.sync.dma_start(w_raw[1][:], w_view[:, :, sum(W_PIECES[:1]):sum(W_PIECES[:2])])
+        nc.sync.dma_start(w_raw[2][:], w_view[:, :, sum(W_PIECES[:2]):sum(W_PIECES[:3])])
+        nc.sync.dma_start(w_raw[3][:], w_view[:, :, sum(W_PIECES[:3]):sum(W_PIECES[:4])])
         nc.sync.dma_start(gate_t[:], gate)
 
         c0 = 0
@@ -82,21 +84,13 @@ def tile_picked_route2_mlprelu_e_kernel(tc, xT, gate, w1, w2_words, w2_scales, o
                                   in_=grouped[:].rearrange("p c j -> p (c j)"))
             c0 = c0 + w
 
-        g_words, g_bytes = [], []
+        half = S // 2
+        gw_early = keep.tile([P, half], U32, name="gw_early", align_bytes=64)
+        gb_early = keep.tile([P, half], U8, name="gb_early", align_bytes=64)
+        nc.vector.tensor_copy(gw_early[:], x_words[:].indirect(offs_t[:, 0:half // 16]))
+        nc.vector.tensor_copy(gb_early[:], x_bytes[:].indirect(offs_t[:, 0:half // 16]))
 
-        def gather(c):
-            gw = keep.tile([P, CH], U32, name="g_words%d" % c, align_bytes=64)
-            gb = keep.tile([P, CH], U8, name="g_bytes%d" % c, align_bytes=64)
-            sl = offs_t[:, c * CH // 16:(c + 1) * CH // 16]
-            nc.vector.tensor_copy(gw[:], x_words[:].indirect(sl))
-            nc.vector.tensor_copy(gb[:], x_bytes[:].indirect(sl))
-            g_words.append(gw)
-            g_bytes.append(gb)
-
-        for c in range(2):
-            gather(c)
-
-        w_grouped = keep.tile([P, PACK, P, PACK], BF16, name="w_grouped", align_bytes=64)
+        w_grouped = late.tile([P, PACK, P, PACK], BF16, name="w_grouped", offset=0, align_bytes=64)
         c0 = 0
         for i, w in enumerate(W_PIECES):
             s = W_SCALAR[i]
@@ -116,14 +110,20 @@ def tile_picked_route2_mlprelu_e_kernel(tc, xT, gate, w1, w2_words, w2_scales, o
             w_words.append(ww)
             w_bytes.append(wb)
 
-        for c in range(2, S // CH):
-            gather(c)
+        gw_late = late.tile([P, half], U32, name="gw_late", offset=0, align_bytes=64)
+        gb_late = [late.tile([P, CH], U8, name="gb_late0", offset=4096, align_bytes=64),
+                   late.tile([P, CH], U8, name="gb_late1", offset=1024, align_bytes=64)]
+        nc.vector.tensor_copy(gb_late[0][:], x_bytes[:].indirect(offs_t[:, 16:24]))
+        nc.vector.tensor_copy(gw_late[:], x_words[:].indirect(offs_t[:, 16:32]))
+        nc.vector.tensor_copy(gb_late[1][:], x_bytes[:].indirect(offs_t[:, 24:32]))
+        g_words = [gw_early[:, 0:CH], gw_early[:, CH:half], gw_late[:, 0:CH], gw_late[:, CH:half]]
+        g_bytes = [gb_early[:, 0:CH], gb_early[:, CH:half], gb_late[0][:], gb_late[1][:]]
 
         def layer1(c):
-            acc = psum.tile([P, PACK, CH], F32, name="h_acc%d" % c)
+            acc = psum.tile([P, PACK, CH], F32, name="h_acc%d" % c, tag=H_BANK[c])
             for t in range(PACK):
                 nc.tensor.matmul_mx(out=acc[:, t, :], lhsT=w_words[t][:].bitcast(FP8X4), lhsT_scale=w_bytes[t][:],
-                                    rhs=g_words[c][:].bitcast(FP8X4), rhs_scale=g_bytes[c][:], start=True, stop=True)
+                                    rhs=g_words[c].bitcast(FP8X4), rhs_scale=g_bytes[c], start=True, stop=True)
             hg = keep.tile([P, CH, PACK], BF16, name="h_grouped%d" % c, align_bytes=64)
             nc.scalar.activation(hg[:], acc[:].rearrange("p t n -> p n t"), RELU)
             return hg
@@ -132,26 +132,29 @@ def tile_picked_route2_mlprelu_e_kernel(tc, xT, gate, w1, w2_words, w2_scales, o
             hw = keep.tile([P, CH], U32, name="h_words%d" % c, align_bytes=64)
             hb = keep.tile([P, CH], U8, name="h_bytes%d" % c, align_bytes=64)
             nc.vector.quantize_mx(out=hw[:].bitcast(FP8X4), scales=hb[:], in_=hg[:].rearrange("p n t -> p (n t)"))
-            acc = psum.tile([P, CH], F32, name="y_acc%d" % c)
+            acc = psum.tile([P, CH], F32, name="y_acc%d" % c, tag=Y_BANK[c])
             nc.tensor.matmul_mx(out=acc[:], lhsT=w2_codes[:].bitcast(FP4X4), lhsT_scale=w2_plane[:],
                                 rhs=hw[:].bitcast(FP8X4), rhs_scale=hb[:], start=True, stop=True)
-            y = keep.tile([P, CH], F32, name="y%d" % c)
-            nc.scalar.activation(y[:], acc[:], COPY)
-            return y
+            return acc
 
-        def scatter(c, y):
-            nc.vector.tensor_tensor(window[:].indirect(dst_t[:, c * CH // 16:(c + 1) * CH // 16]), y[:],
-                                    gate_t[:, c * CH:(c + 1) * CH], MULT)
-
-        n = S // CH
-        hs, ys = {}, {}
-        for step in range(n + 2):
-            if step < n:
-                hs[step] = layer1(step)
-            if 1 <= step <= n:
-                ys[step - 1] = layer2(step - 1, hs[step - 1])
-            if step >= 2:
-                scatter(step - 2, ys[step - 2])
+        y_first = keep.tile([P, CH], F32, name="y_first")
+        y_rest = keep.tile([P, 2 * CH], F32, name="y_rest")
+        y_last = keep.tile([P, CH], F32, name="y_last")
+        h0 = layer1(0)
+        h1 = layer1(1)
+        acc0 = layer2(0, h0)
+        h2 = layer1(2)
+        acc1 = layer2(1, h1)
+        nc.vector.tensor_copy(y_first[:], acc0[:])
+        h3 = layer1(3)
+        acc2 = layer2(2, h2)
+        nc.vector.tensor_tensor(window[:].indirect(dst_t[:, 0:CH // 16]), y_first[:], gate_t[:, 0:CH], MULT)
+        acc3 = layer2(3, h3)
+        for c, acc in enumerate([acc1, acc2]):
+            nc.scalar.activation(y_rest[:, c * CH:(c + 1) * CH], acc[:], COPY)
+        nc.scalar.activation(y_last[:], acc3[:], COPY)
+        nc.vector.tensor_tensor(window[:].indirect(dst_t[:, CH // 16:3 * CH // 16]), y_rest[:], gate_t[:, CH:3 * CH], MULT)
+        nc.vector.tensor_tensor(window[:].indirect(dst_t[:, 3 * CH // 16:S // 16]), y_last[:], gate_t[:, 3 * CH:S], MULT)
 
         nc.sync.dma_start(out[:, 0:U // 2], window[:, 0:U // 2])
         nc.scalar.dma_start(out[:, U // 2:U], window[:, U // 2:U])

@@ -22,7 +22,7 @@ PACK = 4
 X_PIECES = [256,256,256,128,128]
 X_SCALAR = [96,96,96,48,48]
 W_PIECES = [128,128,128,128]
-W_SCALAR = [128,128,128,48]
+W_SCALAR = [128,128,96,32]
 CH = 128
 H_BANK = ["a","b","c","b"]
 Y_BANK = ["e","f","g","h"]
@@ -139,7 +139,7 @@ def tile_picked_route2_mlprelu_e_kernel(tc, xT, gate, w1, w2_words, w2_scales, o
 
         y_first = keep.tile([P, CH], F32, name="y_first")
         y_rest = keep.tile([P, 2 * CH], F32, name="y_rest")
-        y_last = keep.tile([P, CH], F32, name="y_last")
+        y_second = keep.tile([P, CH], F32, name="y_second")
         h0 = layer1(0)
         h1 = layer1(1)
         acc0 = layer2(0, h0)
@@ -150,11 +150,11 @@ def tile_picked_route2_mlprelu_e_kernel(tc, xT, gate, w1, w2_words, w2_scales, o
         acc2 = layer2(2, h2)
         nc.vector.tensor_tensor(window[:].indirect(dst_t[:, 0:CH // 16]), y_first[:], gate_t[:, 0:CH], MULT)
         acc3 = layer2(3, h3)
-        for c, acc in enumerate([acc1, acc2]):
+        nc.scalar.activation(y_second[:], acc1[:], COPY)
+        for c, acc in enumerate([acc2, acc3]):
             nc.scalar.activation(y_rest[:, c * CH:(c + 1) * CH], acc[:], COPY)
-        nc.scalar.activation(y_last[:], acc3[:], COPY)
-        nc.vector.tensor_tensor(window[:].indirect(dst_t[:, CH // 16:3 * CH // 16]), y_rest[:], gate_t[:, CH:3 * CH], MULT)
-        nc.vector.tensor_tensor(window[:].indirect(dst_t[:, 3 * CH // 16:S // 16]), y_last[:], gate_t[:, 3 * CH:S], MULT)
+        nc.vector.tensor_tensor(window[:].indirect(dst_t[:, CH // 16:2 * CH // 16]), y_second[:], gate_t[:, CH:2 * CH], MULT)
+        nc.vector.tensor_tensor(window[:].indirect(dst_t[:, 2 * CH // 16:S // 16]), y_rest[:], gate_t[:, 2 * CH:S], MULT)
 
         nc.sync.dma_start(out[:, 0:U // 2], window[:, 0:U // 2])
         nc.scalar.dma_start(out[:, U // 2:U], window[:, U // 2:U])

@@ -140,7 +140,14 @@ def tile_picked_route2_mlprelu_e_kernel(tc, xT, gate, w1, w2_words, w2_scales, o
         y_first = keep.tile([P, CH], F32, name="y_first")
         y_rest = keep.tile([P, 2 * CH], F32, name="y_rest")
         y_second = keep.tile([P, CH], F32, name="y_second")
-        h0 = layer1(0)
+        h0 = keep.tile([P, CH, PACK], BF16, name="h_grouped0", align_bytes=64)
+        for u in range(2):
+            acc = psum.tile([P, 2, CH], F32, name="h_first%d" % u)
+            for e in range(2):
+                t = 2 * u + e
+                nc.tensor.matmul_mx(out=acc[:, e, :], lhsT=w_words[t][:].bitcast(FP8X4), lhsT_scale=w_bytes[t][:],
+                                    rhs=g_words[0].bitcast(FP8X4), rhs_scale=g_bytes[0], start=True, stop=True)
+            nc.scalar.activation(h0[:, :, 2 * u:2 * u + 2], acc[:].rearrange("p t n -> p n t"), RELU)
         h1 = layer1(1)
         acc0 = layer2(0, h0)
         h2 = layer1(2)

@@ -20,12 +20,14 @@ MULT = mybir.AluOpType.mult
 P = 128
 PACK = 4
 X_PIECES = [256,256,256,128,128]
-X_SCALAR = [96,96,96,48,48]
+X_SCALAR = [160,160,128,128,48]
 W_PIECES = [128,128,128,128]
-W_SCALAR = [128,128,96,32]
+W_SCALAR = [128,128,128,48]
 CH = 128
-H_BANK = ["a","b","c","b"]
-Y_BANK = ["e","f","g","h"]
+HALF_M = P
+RAW_AT = 0
+G_AT = 8192
+H0_AT = 12288
 
 
 def tile_picked_route2_mlprelu_e_kernel(tc, xT, gate, w1, w2_words, w2_scales, offs, dst, out):
@@ -44,6 +46,7 @@ def tile_picked_route2_mlprelu_e_kernel(tc, xT, gate, w1, w2_words, w2_scales, o
         gate_t = keep.tile([P, S], F32, name="gate_t")
         window = keep.tile([P, U], F32, name="window")
 
+
         nc.vector.memset(x_bytes[:].bitcast(I32), 0)
         nc.vector.memset(window[:], 0.0)
 
@@ -51,23 +54,20 @@ def tile_picked_route2_mlprelu_e_kernel(tc, xT, gate, w1, w2_words, w2_scales, o
         w_view = w1.rearrange("(p j) c -> p j c", j=PACK)
         x_raw = [keep.tile([P, PACK, w], F32, name="x_raw%d" % i) for i, w in enumerate(X_PIECES)]
         w_raw = [keep.tile([P, PACK, w], F32, name="w_raw%d" % i) for i, w in enumerate(W_PIECES[:-1])]
-        w_raw.append(late.tile([P, PACK, W_PIECES[-1]], F32, name="w_raw_last", offset=4096, align_bytes=64))
-        nc.sync.dma_start(x_raw[0][:], x_view[:, :, sum(X_PIECES[:0]):sum(X_PIECES[:1])])
-        nc.sync.dma_start(w2_plane[0:4, :].bitcast(I32), w2_scales[0, 0:4, :].bitcast(I32))
-        nc.sync.dma_start(w2_plane[32:36, :].bitcast(I32), w2_scales[0, 4:8, :].bitcast(I32))
-        nc.sync.dma_start(w2_plane[64:68, :].bitcast(I32), w2_scales[0, 8:12, :].bitcast(I32))
-        nc.sync.dma_start(w2_plane[96:100, :].bitcast(I32), w2_scales[0, 12:16, :].bitcast(I32))
+        w_raw.append(late.tile([P, PACK, W_PIECES[-1]], F32, name="w_raw_last", offset=RAW_AT, align_bytes=64))
+
+        def load_w2(queue):
+            queue.dma_start(w2_codes[:].bitcast(I32), w2_words[0].bitcast(I32))
+            for q in range(4):
+                queue.dma_start(w2_plane[32 * q:32 * q + 4, :].bitcast(I32), w2_scales[0, 4 * q:4 * q + 4, :].bitcast(I32))
+
+        for i in range(len(X_PIECES)):
+            nc.sync.dma_start(x_raw[i][:], x_view[:, :, sum(X_PIECES[:i]):sum(X_PIECES[:i + 1])])
         nc.sync.dma_start(offs_t[:], offs)
-        nc.sync.dma_start(x_raw[1][:], x_view[:, :, sum(X_PIECES[:1]):sum(X_PIECES[:2])])
-        nc.sync.dma_start(x_raw[2][:], x_view[:, :, sum(X_PIECES[:2]):sum(X_PIECES[:3])])
-        nc.sync.dma_start(x_raw[3][:], x_view[:, :, sum(X_PIECES[:3]):sum(X_PIECES[:4])])
-        nc.sync.dma_start(x_raw[4][:], x_view[:, :, sum(X_PIECES[:4]):sum(X_PIECES[:5])])
-        nc.sync.dma_start(w2_codes[:].bitcast(I32), w2_words[0].bitcast(I32))
+        for i in range(len(W_PIECES)):
+            nc.sync.dma_start(w_raw[i][:], w_view[:, :, sum(W_PIECES[:i]):sum(W_PIECES[:i + 1])])
+        load_w2(nc.sync)
         nc.sync.dma_start(dst_t[:], dst)
-        nc.sync.dma_start(w_raw[0][:], w_view[:, :, sum(W_PIECES[:0]):sum(W_PIECES[:1])])
-        nc.sync.dma_start(w_raw[1][:], w_view[:, :, sum(W_PIECES[:1]):sum(W_PIECES[:2])])
-        nc.sync.dma_start(w_raw[2][:], w_view[:, :, sum(W_PIECES[:2]):sum(W_PIECES[:3])])
-        nc.sync.dma_start(w_raw[3][:], w_view[:, :, sum(W_PIECES[:3]):sum(W_PIECES[:4])])
         nc.sync.dma_start(gate_t[:], gate)
 
         c0 = 0
@@ -84,46 +84,51 @@ def tile_picked_route2_mlprelu_e_kernel(tc, xT, gate, w1, w2_words, w2_scales, o
                                   in_=grouped[:].rearrange("p c j -> p (c j)"))
             c0 = c0 + w
 
-        half = S // 2
-        gw_early = keep.tile([P, half], U32, name="gw_early", align_bytes=64)
-        gb_early = keep.tile([P, half], U8, name="gb_early", align_bytes=64)
-        nc.vector.tensor_copy(gw_early[:], x_words[:].indirect(offs_t[:, 0:half // 16]))
-        nc.vector.tensor_copy(gb_early[:], x_bytes[:].indirect(offs_t[:, 0:half // 16]))
+        cols = CH // 16
 
-        w_grouped = late.tile([P, PACK, P, PACK], BF16, name="w_grouped", offset=0, align_bytes=64)
+        def gather(tile, source, c):
+            nc.vector.tensor_copy(tile[:], source[:].indirect(offs_t[:, c * cols:(c + 1) * cols]))
+
+        gw_early = keep.tile([P, 2 * CH], U32, name="gw_early", align_bytes=64)
+        gb_early = keep.tile([P, 2 * CH], U8, name="gb_early", align_bytes=64)
+        nc.vector.tensor_copy(gw_early[:], x_words[:].indirect(offs_t[:, 0:2 * cols]))
+        nc.vector.tensor_copy(gb_early[:], x_bytes[:].indirect(offs_t[:, 0:2 * cols]))
+        gw0, gb0, gw1, gb1 = gw_early[:, 0:CH], gb_early[:, 0:CH], gw_early[:, CH:2 * CH], gb_early[:, CH:2 * CH]
+
+        w_words = [keep.tile([P, P], U32, name="w_words%d" % t, align_bytes=64) for t in range(PACK)]
+        w_bytes = [keep.tile([P, P], U8, name="w_bytes%d" % t, align_bytes=64) for t in range(PACK)]
+        w_grouped = [keep.tile([P, PACK, HALF_M, PACK], BF16, name="w_grouped%d" % u, align_bytes=64) for u in range(1)]
         c0 = 0
         for i, w in enumerate(W_PIECES):
             s = W_SCALAR[i]
+            u, m0 = divmod(c0 // PACK, HALF_M)
             if s > 0:
-                nc.scalar.activation(w_grouped[:, :, c0 // 4:(c0 + s) // 4, :].rearrange("p t m j -> p m j t"),
+                nc.scalar.activation(w_grouped[u][:, :, m0:m0 + s // 4, :].rearrange("p t m j -> p m j t"),
                                      w_raw[i][:, :, 0:s].rearrange("p j (m t) -> p m j t", t=4), COPY)
             if s < w:
-                nc.vector.tensor_copy(w_grouped[:, :, (c0 + s) // 4:(c0 + w) // 4, :].rearrange("p t m j -> p m j t"),
+                nc.vector.tensor_copy(w_grouped[u][:, :, m0 + s // 4:m0 + w // 4, :].rearrange("p t m j -> p m j t"),
                                       w_raw[i][:, :, s:w].rearrange("p j (m t) -> p m j t", t=4))
             c0 = c0 + w
-        w_words, w_bytes = [], []
-        for t in range(PACK):
-            ww = keep.tile([P, P], U32, name="w_words%d" % t, align_bytes=64)
-            wb = keep.tile([P, P], U8, name="w_bytes%d" % t, align_bytes=64)
-            nc.vector.quantize_mx(out=ww[:].bitcast(FP8X4), scales=wb[:],
-                                  in_=w_grouped[:, t, :, :].rearrange("p m j -> p (m j)"))
-            w_words.append(ww)
-            w_bytes.append(wb)
+            if c0 % H == 0:
+                for t in range(PACK):
+                    nc.vector.quantize_mx(out=w_words[t][:, u * HALF_M:(u + 1) * HALF_M].bitcast(FP8X4),
+                                          scales=w_bytes[t][:, u * HALF_M:(u + 1) * HALF_M],
+                                          in_=w_grouped[u][:, t, :, :].rearrange("p m j -> p (m j)"))
 
-        gw_late = late.tile([P, half], U32, name="gw_late", offset=0, align_bytes=64)
-        gb_late = [late.tile([P, CH], U8, name="gb_late0", offset=4096, align_bytes=64),
-                   late.tile([P, CH], U8, name="gb_late1", offset=1024, align_bytes=64)]
-        nc.vector.tensor_copy(gb_late[0][:], x_bytes[:].indirect(offs_t[:, 16:24]))
-        nc.vector.tensor_copy(gw_late[:], x_words[:].indirect(offs_t[:, 16:32]))
-        nc.vector.tensor_copy(gb_late[1][:], x_bytes[:].indirect(offs_t[:, 24:32]))
-        g_words = [gw_early[:, 0:CH], gw_early[:, CH:half], gw_late[:, 0:CH], gw_late[:, CH:half]]
-        g_bytes = [gb_early[:, 0:CH], gb_early[:, CH:half], gb_late[0][:], gb_late[1][:]]
+        gw2 = late.tile([P, CH], U32, name="gw2", offset=RAW_AT, align_bytes=64)
+        gb2 = late.tile([P, CH], U8, name="gb2", offset=RAW_AT + 512, align_bytes=64)
+        gw3 = late.tile([P, CH], U32, name="gw3", offset=RAW_AT + 1024, align_bytes=64)
+        gb3 = late.tile([P, CH], U8, name="gb3", offset=RAW_AT + 640, align_bytes=64)
+        gather(gw2, x_words, 2)
+        gather(gb2, x_bytes, 2)
+        gather(gw3, x_words, 3)
+        gather(gb3, x_bytes, 3)
 
-        def layer1(c):
-            acc = psum.tile([P, PACK, CH], F32, name="h_acc%d" % c, tag=H_BANK[c])
+        def layer1(c, gw, gb, tag):
+            acc = psum.tile([P, PACK, CH], F32, name="h_acc%d" % c, tag=tag)
             for t in range(PACK):
                 nc.tensor.matmul_mx(out=acc[:, t, :], lhsT=w_words[t][:].bitcast(FP8X4), lhsT_scale=w_bytes[t][:],
-                                    rhs=g_words[c].bitcast(FP8X4), rhs_scale=g_bytes[c], start=True, stop=True)
+                                    rhs=gw.bitcast(FP8X4), rhs_scale=gb, start=True, stop=True)
             hg = keep.tile([P, CH, PACK], BF16, name="h_grouped%d" % c, align_bytes=64)
             nc.scalar.activation(hg[:], acc[:].rearrange("p t n -> p n t"), RELU)
             return hg
@@ -132,36 +137,69 @@ def tile_picked_route2_mlprelu_e_kernel(tc, xT, gate, w1, w2_words, w2_scales, o
             hw = keep.tile([P, CH], U32, name="h_words%d" % c, align_bytes=64)
             hb = keep.tile([P, CH], U8, name="h_bytes%d" % c, align_bytes=64)
             nc.vector.quantize_mx(out=hw[:].bitcast(FP8X4), scales=hb[:], in_=hg[:].rearrange("p n t -> p (n t)"))
-            acc = psum.tile([P, CH], F32, name="y_acc%d" % c, tag=Y_BANK[c])
+
+            acc = psum.tile([P, CH], F32, name="y_acc%d" % c, tag=["y0", "y1", "y2", "b"][c])
             nc.tensor.matmul_mx(out=acc[:], lhsT=w2_codes[:].bitcast(FP4X4), lhsT_scale=w2_plane[:],
                                 rhs=hw[:].bitcast(FP8X4), rhs_scale=hb[:], start=True, stop=True)
             return acc
 
-        y_first = keep.tile([P, CH], F32, name="y_first")
-        y_rest = keep.tile([P, 2 * CH], F32, name="y_rest")
-        y_second = keep.tile([P, CH], F32, name="y_second")
-        h0 = keep.tile([P, CH, PACK], BF16, name="h_grouped0", align_bytes=64)
+        h0 = late.tile([P, CH, PACK], BF16, name="h_grouped0", offset=H0_AT, align_bytes=64)
         for u in range(2):
-            acc = psum.tile([P, 2, CH], F32, name="h_first%d" % u)
+            acc = psum.tile([P, 2, CH], F32, name="h_first%d" % u, tag="a%d" % u)
             for e in range(2):
                 t = 2 * u + e
                 nc.tensor.matmul_mx(out=acc[:, e, :], lhsT=w_words[t][:].bitcast(FP8X4), lhsT_scale=w_bytes[t][:],
-                                    rhs=g_words[0].bitcast(FP8X4), rhs_scale=g_bytes[0], start=True, stop=True)
+                                    rhs=gw0.bitcast(FP8X4), rhs_scale=gb0, start=True, stop=True)
             nc.scalar.activation(h0[:, :, 2 * u:2 * u + 2], acc[:].rearrange("p t n -> p n t"), RELU)
-        h1 = layer1(1)
+        h1 = layer1(1, gw1, gb1, "b")
         acc0 = layer2(0, h0)
-        h2 = layer1(2)
+        h2 = keep.tile([P, CH, PACK], BF16, name="h_grouped2", align_bytes=64)
+        for u in range(2):
+            acc = psum.tile([P, 2, CH], F32, name="h_third%d" % u, tag="c%d" % u)
+            for e in range(2):
+                t = 2 * u + e
+                nc.tensor.matmul_mx(out=acc[:, e, :], lhsT=w_words[t][:].bitcast(FP8X4), lhsT_scale=w_bytes[t][:],
+                                    rhs=gw2[:].bitcast(FP8X4), rhs_scale=gb2[:], start=True, stop=True)
+            if u == 0:
+                nc.scalar.activation(h2[:, :, 2 * u:2 * u + 2], acc[:].rearrange("p t n -> p n t"), RELU)
+            else:
+                nc.vector.tensor_scalar_max(h2[:, :, 2 * u:2 * u + 2], acc[:].rearrange("p t n -> p n t"), 0.0)
         acc1 = layer2(1, h1)
-        nc.vector.tensor_copy(y_first[:], acc0[:])
-        h3 = layer1(3)
+        groups = [1,3]
+        y_tiles = [keep.tile([P, g * CH], F32, name="y%d" % i) for i, g in enumerate(groups)]
+        places = [(i, e) for i, g in enumerate(groups) for e in range(g)]
+
+        def empty(c, acc):
+            i, e = places[c]
+            if c == 0 and False:
+                nc.vector.tensor_copy(y_tiles[i][:, e * CH:(e + 1) * CH], acc[:])
+            else:
+                nc.scalar.activation(y_tiles[i][:, e * CH:(e + 1) * CH], acc[:], COPY)
+
+
+        def scatter(i):
+            a, b = sum(groups[:i]), sum(groups[:i + 1])
+            nc.vector.tensor_tensor(window[:].indirect(dst_t[:, a * cols:b * cols]), y_tiles[i][:], gate_t[:, a * CH:b * CH], MULT)
+
+        h3 = keep.tile([P, CH, PACK], BF16, name="h_grouped3", align_bytes=64)
+        for u in range(2):
+            acc = psum.tile([P, 2, CH], F32, name="h_last%d" % u, tag="a%d" % u)
+            for e in range(2):
+                t = 2 * u + e
+                nc.tensor.matmul_mx(out=acc[:, e, :], lhsT=w_words[t][:].bitcast(FP8X4), lhsT_scale=w_bytes[t][:],
+                                    rhs=gw3[:].bitcast(FP8X4), rhs_scale=gb3[:], start=True, stop=True)
+            if u == 0 or True:
+                nc.scalar.activation(h3[:, :, 2 * u:2 * u + 2], acc[:].rearrange("p t n -> p n t"), RELU)
+            else:
+                nc.vector.tensor_scalar_max(h3[:, :, 2 * u:2 * u + 2], acc[:].rearrange("p t n -> p n t"), 0.0)
         acc2 = layer2(2, h2)
-        nc.vector.tensor_tensor(window[:].indirect(dst_t[:, 0:CH // 16]), y_first[:], gate_t[:, 0:CH], MULT)
+        empty(0, acc0)
         acc3 = layer2(3, h3)
-        nc.scalar.activation(y_second[:], acc1[:], COPY)
-        for c, acc in enumerate([acc2, acc3]):
-            nc.scalar.activation(y_rest[:, c * CH:(c + 1) * CH], acc[:], COPY)
-        nc.vector.tensor_tensor(window[:].indirect(dst_t[:, CH // 16:2 * CH // 16]), y_second[:], gate_t[:, CH:2 * CH], MULT)
-        nc.vector.tensor_tensor(window[:].indirect(dst_t[:, 2 * CH // 16:S // 16]), y_rest[:], gate_t[:, 2 * CH:S], MULT)
+        empty(1, acc1)
+        empty(2, acc2)
+        empty(3, acc3)
+        for i in range(len(groups)):
+            scatter(i)
 
         nc.sync.dma_start(out[:, 0:U // 2], window[:, 0:U // 2])
         nc.scalar.dma_start(out[:, U // 2:U], window[:, U // 2:U])

@@ -22,12 +22,13 @@ PACK = 4
 X_PIECES = [256,256,256,128,128]
 X_SCALAR = [160,160,128,128,48]
 W_PIECES = [128,128,128,128]
-W_SCALAR = [128,128,128,48]
+W_SCALAR = [128,128,128,32]
 CH = 128
 HALF_M = P
 RAW_AT = 0
 G_AT = 8192
 H0_AT = 12288
+Q_AT = 16384
 
 
 def tile_picked_route2_mlprelu_e_kernel(tc, xT, gate, w1, w2_words, w2_scales, offs, dst, out):
@@ -119,87 +120,67 @@ def tile_picked_route2_mlprelu_e_kernel(tc, xT, gate, w1, w2_words, w2_scales, o
         gb2 = late.tile([P, CH], U8, name="gb2", offset=RAW_AT + 512, align_bytes=64)
         gw3 = late.tile([P, CH], U32, name="gw3", offset=RAW_AT + 1024, align_bytes=64)
         gb3 = late.tile([P, CH], U8, name="gb3", offset=RAW_AT + 640, align_bytes=64)
-        gather(gw2, x_words, 2)
-        gather(gb2, x_bytes, 2)
-        gather(gw3, x_words, 3)
-        gather(gb3, x_bytes, 3)
-
-        def layer1(c, gw, gb, tag):
-            acc = psum.tile([P, PACK, CH], F32, name="h_acc%d" % c, tag=tag)
-            for t in range(PACK):
-                nc.tensor.matmul_mx(out=acc[:, t, :], lhsT=w_words[t][:].bitcast(FP8X4), lhsT_scale=w_bytes[t][:],
-                                    rhs=gw.bitcast(FP8X4), rhs_scale=gb, start=True, stop=True)
-            hg = keep.tile([P, CH, PACK], BF16, name="h_grouped%d" % c, align_bytes=64)
-            nc.scalar.activation(hg[:], acc[:].rearrange("p t n -> p n t"), RELU)
-            return hg
-
-        def layer2(c, hg):
-            hw = keep.tile([P, CH], U32, name="h_words%d" % c, align_bytes=64)
-            hb = keep.tile([P, CH], U8, name="h_bytes%d" % c, align_bytes=64)
-            nc.vector.quantize_mx(out=hw[:].bitcast(FP8X4), scales=hb[:], in_=hg[:].rearrange("p n t -> p (n t)"))
-
-            acc = psum.tile([P, CH], F32, name="y_acc%d" % c, tag=["y0", "y1", "y2", "b"][c])
-            nc.tensor.matmul_mx(out=acc[:], lhsT=w2_codes[:].bitcast(FP4X4), lhsT_scale=w2_plane[:],
-                                rhs=hw[:].bitcast(FP8X4), rhs_scale=hb[:], start=True, stop=True)
-            return acc
-
-        h0 = late.tile([P, CH, PACK], BF16, name="h_grouped0", offset=H0_AT, align_bytes=64)
-        for u in range(2):
-            acc = psum.tile([P, 2, CH], F32, name="h_first%d" % u, tag="a%d" % u)
-            for e in range(2):
-                t = 2 * u + e
-                nc.tensor.matmul_mx(out=acc[:, e, :], lhsT=w_words[t][:].bitcast(FP8X4), lhsT_scale=w_bytes[t][:],
-                                    rhs=gw0.bitcast(FP8X4), rhs_scale=gb0, start=True, stop=True)
-            nc.scalar.activation(h0[:, :, 2 * u:2 * u + 2], acc[:].rearrange("p t n -> p n t"), RELU)
-        h1 = layer1(1, gw1, gb1, "b")
-        acc0 = layer2(0, h0)
-        h2 = keep.tile([P, CH, PACK], BF16, name="h_grouped2", align_bytes=64)
-        for u in range(2):
-            acc = psum.tile([P, 2, CH], F32, name="h_third%d" % u, tag="c%d" % u)
-            for e in range(2):
-                t = 2 * u + e
-                nc.tensor.matmul_mx(out=acc[:, e, :], lhsT=w_words[t][:].bitcast(FP8X4), lhsT_scale=w_bytes[t][:],
-                                    rhs=gw2[:].bitcast(FP8X4), rhs_scale=gb2[:], start=True, stop=True)
-            if u == 0:
-                nc.scalar.activation(h2[:, :, 2 * u:2 * u + 2], acc[:].rearrange("p t n -> p n t"), RELU)
-            else:
-                nc.vector.tensor_scalar_max(h2[:, :, 2 * u:2 * u + 2], acc[:].rearrange("p t n -> p n t"), 0.0)
-        acc1 = layer2(1, h1)
+        g_words = [gw0, gw1, gw2[:], gw3[:]]
+        g_bytes = [gb0, gb1, gb2[:], gb3[:]]
+        h_grouped = [late.tile([P, CH, PACK], BF16, name="h_grouped%d" % c, offset=H0_AT + 1024 * c, align_bytes=64) for c in range(4)]
+        h_words = [late.tile([P, CH], U32, name="h_words%d" % c, offset=Q_AT + [0, 1024, 2048, 3072][c], align_bytes=64) for c in range(4)]
+        h_bytes = [late.tile([P, CH], U8, name="h_bytes%d" % c, offset=Q_AT + [512, 1536, 2560, 3584][c], align_bytes=64) for c in range(4)]
         groups = [1,3]
         y_tiles = [keep.tile([P, g * CH], F32, name="y%d" % i) for i, g in enumerate(groups)]
         places = [(i, e) for i, g in enumerate(groups) for e in range(g)]
 
-        def empty(c, acc):
-            i, e = places[c]
-            if c == 0 and False:
-                nc.vector.tensor_copy(y_tiles[i][:, e * CH:(e + 1) * CH], acc[:])
-            else:
-                nc.scalar.activation(y_tiles[i][:, e * CH:(e + 1) * CH], acc[:], COPY)
+        def first(c, t0, t1, tag):
+            acc = psum.tile([P, t1 - t0, CH], F32, name="h_acc%d_%d" % (c, t0), tag=tag)
+            for t in range(t0, t1):
+                nc.tensor.matmul_mx(out=acc[:, t - t0, :], lhsT=w_words[t][:].bitcast(FP8X4), lhsT_scale=w_bytes[t][:],
+                                    rhs=g_words[c].bitcast(FP8X4), rhs_scale=g_bytes[c], start=True, stop=True)
+            return acc
 
+        def relu_s(c, t0, t1, acc):
+            nc.scalar.activation(h_grouped[c][:, :, t0:t1], acc[:].rearrange("p t n -> p n t"), RELU)
+
+        def relu_v(c, t0, t1, acc):
+            nc.vector.tensor_scalar_max(h_grouped[c][:, :, t0:t1], acc[:].rearrange("p t n -> p n t"), 0.0)
+
+        def quant(c):
+            nc.vector.quantize_mx(out=h_words[c][:].bitcast(FP8X4), scales=h_bytes[c][:], in_=h_grouped[c][:].rearrange("p n t -> p (n t)"))
+
+        def second(c, tag):
+            acc = psum.tile([P, CH], F32, name="y_acc%d" % c, tag=tag)
+            nc.tensor.matmul_mx(out=acc[:], lhsT=w2_codes[:].bitcast(FP4X4), lhsT_scale=w2_plane[:],
+                                rhs=h_words[c][:].bitcast(FP8X4), rhs_scale=h_bytes[c][:], start=True, stop=True)
+            return acc
+
+        def empty_s(c, acc):
+            i, e = places[c]
+            nc.scalar.activation(y_tiles[i][:, e * CH:(e + 1) * CH], acc[:], COPY)
+
+        def empty_v(c, acc):
+            i, e = places[c]
+            nc.vector.tensor_copy(y_tiles[i][:, e * CH:(e + 1) * CH], acc[:])
 
         def scatter(i):
             a, b = sum(groups[:i]), sum(groups[:i + 1])
             nc.vector.tensor_tensor(window[:].indirect(dst_t[:, a * cols:b * cols]), y_tiles[i][:], gate_t[:, a * CH:b * CH], MULT)
 
-        h3 = keep.tile([P, CH, PACK], BF16, name="h_grouped3", align_bytes=64)
-        for u in range(2):
-            acc = psum.tile([P, 2, CH], F32, name="h_last%d" % u, tag="a%d" % u)
-            for e in range(2):
-                t = 2 * u + e
-                nc.tensor.matmul_mx(out=acc[:, e, :], lhsT=w_words[t][:].bitcast(FP8X4), lhsT_scale=w_bytes[t][:],
-                                    rhs=gw3[:].bitcast(FP8X4), rhs_scale=gb3[:], start=True, stop=True)
-            if u == 0 or True:
-                nc.scalar.activation(h3[:, :, 2 * u:2 * u + 2], acc[:].rearrange("p t n -> p n t"), RELU)
-            else:
-                nc.vector.tensor_scalar_max(h3[:, :, 2 * u:2 * u + 2], acc[:].rearrange("p t n -> p n t"), 0.0)
-        acc2 = layer2(2, h2)
-        empty(0, acc0)
-        acc3 = layer2(3, h3)
-        empty(1, acc1)
-        empty(2, acc2)
-        empty(3, acc3)
-        for i in range(len(groups)):
-            scatter(i)
+        gather(gw2, x_words, 2)
+        gather(gb2, x_bytes, 2)
+        gather(gw3, x_words, 3)
+        gather(gb3, x_bytes, 3)
+        relu_s(0, 0, 4, first(0, 0, 4, "a0"))
+        relu_s(1, 0, 4, first(1, 0, 4, "b"))
+        quant(0)
+        relu_v(2, 0, 4, first(2, 0, 4, "c0"))
+        quant(1)
+        relu_s(3, 0, 4, first(3, 0, 4, "a1"))
+        quant(2)
+        empty_s(0, second(0, "y0"))
+        quant(3)
+        scatter(0)
+        empty_s(1, second(1, "y1"))
+        empty_s(2, second(2, "y2"))
+        empty_s(3, second(3, "y3"))
+        scatter(1)
 
         nc.sync.dma_start(out[:, 0:U // 2], window[:, 0:U // 2])
         nc.scalar.dma_start(out[:, U // 2:U], window[:, U // 2:U])

@@ -90,10 +90,17 @@ def tile_picked_route2_mlprelu_e_kernel(tc, xT, gate, w1, w2_words, w2_scales, o
         def gather(tile, source, c):
             nc.vector.tensor_copy(tile[:], source[:].indirect(offs_t[:, c * cols:(c + 1) * cols]))
 
-        gw_early = keep.tile([P, 2 * CH], U32, name="gw_early", align_bytes=64)
-        gb_early = keep.tile([P, 2 * CH], U8, name="gb_early", align_bytes=64)
-        nc.vector.tensor_copy(gw_early[:], x_words[:].indirect(offs_t[:, 0:2 * cols]))
-        nc.vector.tensor_copy(gb_early[:], x_bytes[:].indirect(offs_t[:, 0:2 * cols]))
+        gw_wide = keep.tile([P, 4 * CH], I32, name="gw_early", align_bytes=64)
+        gb_early = keep.tile([P, 4 * CH], U8, name="gb_early", align_bytes=64)
+        nc.vector.memset(gw_wide[:, 2 * CH:4 * CH], 0)
+        nc.vector.memset(gb_early[:, 2 * CH:4 * CH].bitcast(I32), 0)
+        gw_early = gw_wide[:].bitcast(U32)
+        nc.vector.tensor_copy(gw_early[:, 0:2 * CH], x_words[:].indirect(offs_t[:, 0:2 * cols]))
+        nc.vector.tensor_copy(gb_early[:, 0:2 * CH], x_bytes[:].indirect(offs_t[:, 0:2 * cols]))
+        for u in range(2):
+            warm = psum.tile([32, 4 * CH], F32, name="warm%d" % u, tag="y%d" % (2 + u))
+            nc.tensor.matmul_mx(out=warm[:], lhsT=gw_early[:, 0:32].bitcast(FP8X4), lhsT_scale=gb_early[:, 0:32],
+                                rhs=gw_early.bitcast(FP8X4), rhs_scale=gb_early[:], start=True, stop=True)
         gw0, gb0, gw1, gb1 = gw_early[:, 0:CH], gb_early[:, 0:CH], gw_early[:, CH:2 * CH], gb_early[:, CH:2 * CH]
 
         w_words = [keep.tile([P, P], U32, name="w_words%d" % t, align_bytes=64) for t in range(PACK)]

@@ -22,9 +22,9 @@ PACK = 4
 X_PIECES = [256,256,256,128,128]
 X_SCALAR = [160,160,128,128,48]
 W_PIECES = [128,128,128,128]
-W_SCALAR = [128,128,128,32]
+W_SCALAR = [128,128,128,64]
 CH = 128
-HALF_M = P
+HALF_M = P // 2
 RAW_AT = 0
 G_AT = 8192
 H0_AT = 12288
@@ -92,20 +92,25 @@ def tile_picked_route2_mlprelu_e_kernel(tc, xT, gate, w1, w2_words, w2_scales, o
 
         gw_wide = keep.tile([P, 4 * CH], I32, name="gw_early", align_bytes=64)
         gb_early = keep.tile([P, 4 * CH], U8, name="gb_early", align_bytes=64)
-        nc.vector.memset(gw_wide[:, 2 * CH:4 * CH], 0)
-        nc.vector.memset(gb_early[:, 2 * CH:4 * CH].bitcast(I32), 0)
+        nc.vector.memset(gw_wide[:, CH:4 * CH], 0)
+        nc.vector.memset(gb_early[:, CH:4 * CH].bitcast(I32), 0)
         gw_early = gw_wide[:].bitcast(U32)
-        nc.vector.tensor_copy(gw_early[:, 0:2 * CH], x_words[:].indirect(offs_t[:, 0:2 * cols]))
-        nc.vector.tensor_copy(gb_early[:, 0:2 * CH], x_bytes[:].indirect(offs_t[:, 0:2 * cols]))
+        gw0, gb0 = gw_early[:, 0:CH], gb_early[:, 0:CH]
+        nc.vector.tensor_copy(gw0, x_words[:].indirect(offs_t[:, 0:cols]))
+        nc.vector.tensor_copy(gb0, x_bytes[:].indirect(offs_t[:, 0:cols]))
         for u in range(2):
             warm = psum.tile([32, 4 * CH], F32, name="warm%d" % u, tag="y%d" % (2 + u))
             nc.tensor.matmul_mx(out=warm[:], lhsT=gw_early[:, 0:32].bitcast(FP8X4), lhsT_scale=gb_early[:, 0:32],
                                 rhs=gw_early.bitcast(FP8X4), rhs_scale=gb_early[:], start=True, stop=True)
-        gw0, gb0, gw1, gb1 = gw_early[:, 0:CH], gb_early[:, 0:CH], gw_early[:, CH:2 * CH], gb_early[:, CH:2 * CH]
+        gw1_t = keep.tile([P, CH], U32, name="gw1", align_bytes=64)
+        gb1_t = keep.tile([P, CH], U8, name="gb1", align_bytes=64)
+        gather(gw1_t, x_words, 1)
+        gather(gb1_t, x_bytes, 1)
+        gw1, gb1 = gw1_t[:], gb1_t[:]
 
         w_words = [keep.tile([P, P], U32, name="w_words%d" % t, align_bytes=64) for t in range(PACK)]
         w_bytes = [keep.tile([P, P], U8, name="w_bytes%d" % t, align_bytes=64) for t in range(PACK)]
-        w_grouped = [keep.tile([P, PACK, HALF_M, PACK], BF16, name="w_grouped%d" % u, align_bytes=64) for u in range(1)]
+        w_grouped = [keep.tile([P, PACK, HALF_M, PACK], BF16, name="w_grouped%d" % u, align_bytes=64) for u in range(2)]
         c0 = 0
         for i, w in enumerate(W_PIECES):
             s = W_SCALAR[i]
@@ -117,7 +122,7 @@ def tile_picked_route2_mlprelu_e_kernel(tc, xT, gate, w1, w2_words, w2_scales, o
                 nc.vector.tensor_copy(w_grouped[u][:, :, m0 + s // 4:m0 + w // 4, :].rearrange("p t m j -> p m j t"),
                                       w_raw[i][:, :, s:w].rearrange("p j (m t) -> p m j t", t=4))
             c0 = c0 + w
-            if c0 % H == 0:
+            if c0 % (H // 2) == 0:
                 for t in range(PACK):
                     nc.vector.quantize_mx(out=w_words[t][:, u * HALF_M:(u + 1) * HALF_M].bitcast(FP8X4),
                                           scales=w_bytes[t][:, u * HALF_M:(u + 1) * HALF_M],

@@ -19,13 +19,15 @@ MULT = mybir.AluOpType.mult
 
 P = 128
 PACK = 4
+X_LOADS = [256,256,256,128,128]
 X_PIECES = [256,256,256,128,128]
 X_SCALAR = [160,160,128,128,48]
 W_PIECES = [128,128,128,128]
-W_SCALAR = [128,128,128,64]
+W_SCALAR = [128,128,128,40]
 CH = 128
 HALF_M = P // 2
 RAW_AT = 0
+THIRD_AT = 2048
 G_AT = 8192
 H0_AT = 12288
 Q_AT = 16384
@@ -53,8 +55,9 @@ def tile_picked_route2_mlprelu_e_kernel(tc, xT, gate, w1, w2_words, w2_scales, o
 
         x_view = xT.rearrange("(p j) t -> p j t", j=PACK)
         w_view = w1.rearrange("(p j) c -> p j c", j=PACK)
-        x_raw = [keep.tile([P, PACK, w], F32, name="x_raw%d" % i) for i, w in enumerate(X_PIECES)]
-        w_raw = [keep.tile([P, PACK, w], F32, name="w_raw%d" % i) for i, w in enumerate(W_PIECES[:-1])]
+        x_raw = [keep.tile([P, PACK, w], F32, name="x_raw%d" % i) for i, w in enumerate(X_LOADS)]
+        w_raw = [keep.tile([P, PACK, w], F32, name="w_raw%d" % i) for i, w in enumerate(W_PIECES[:-2])]
+        w_raw.append(late.tile([P, PACK, W_PIECES[-2]], F32, name="w_raw_third", offset=THIRD_AT, align_bytes=64))
         w_raw.append(late.tile([P, PACK, W_PIECES[-1]], F32, name="w_raw_last", offset=RAW_AT, align_bytes=64))
 
         def load_w2(queue):
@@ -62,8 +65,8 @@ def tile_picked_route2_mlprelu_e_kernel(tc, xT, gate, w1, w2_words, w2_scales, o
             for q in range(4):
                 queue.dma_start(w2_plane[32 * q:32 * q + 4, :].bitcast(I32), w2_scales[0, 4 * q:4 * q + 4, :].bitcast(I32))
 
-        for i in range(len(X_PIECES)):
-            nc.sync.dma_start(x_raw[i][:], x_view[:, :, sum(X_PIECES[:i]):sum(X_PIECES[:i + 1])])
+        for i in range(len(X_LOADS)):
+            nc.sync.dma_start(x_raw[i][:], x_view[:, :, sum(X_LOADS[:i]):sum(X_LOADS[:i + 1])])
         nc.sync.dma_start(offs_t[:], offs)
         for i in range(len(W_PIECES)):
             nc.sync.dma_start(w_raw[i][:], w_view[:, :, sum(W_PIECES[:i]):sum(W_PIECES[:i + 1])])
@@ -71,19 +74,21 @@ def tile_picked_route2_mlprelu_e_kernel(tc, xT, gate, w1, w2_words, w2_scales, o
         nc.sync.dma_start(dst_t[:], dst)
         nc.sync.dma_start(gate_t[:], gate)
 
-        c0 = 0
-        for i, w in enumerate(X_PIECES):
-            grouped = keep.tile([P, w, PACK], BF16, name="x_grouped%d" % i, align_bytes=64)
-            s = X_SCALAR[i]
-            if s > 0:
-                nc.scalar.activation(grouped[:, 0:s, :].rearrange("p (c i) j -> p c j i", i=4),
-                                     x_raw[i][:, :, 0:s].rearrange("p j (c i) -> p c j i", i=4), COPY)
-            if s < w:
-                nc.vector.tensor_copy(grouped[:, s:w, :].rearrange("p (c i) j -> p c j i", i=4),
-                                      x_raw[i][:, :, s:w].rearrange("p j (c i) -> p c j i", i=4))
-            nc.vector.quantize_mx(out=x_words[:, c0:c0 + w].bitcast(FP8X4), scales=x_bytes[:, c0:c0 + w],
-                                  in_=grouped[:].rearrange("p c j -> p (c j)"))
-            c0 = c0 + w
+        x_grouped = [keep.tile([P, w, PACK], BF16, name="x_grouped%d" % i, align_bytes=64) for i, w in enumerate(X_PIECES)]
+        for load in range(len(X_LOADS)):
+            first_token = sum(X_LOADS[:load])
+            pieces = [i for i in range(len(X_PIECES)) if first_token <= sum(X_PIECES[:i]) < first_token + X_LOADS[load]]
+            for i in pieces:
+                a, s, w = sum(X_PIECES[:i]) - first_token, X_SCALAR[i], X_PIECES[i]
+                nc.scalar.activation(x_grouped[i][:, 0:s, :].rearrange("p (c i) j -> p c j i", i=4),
+                                     x_raw[load][:, :, a:a + s].rearrange("p j (c i) -> p c j i", i=4), COPY)
+                if s < w:
+                    nc.vector.tensor_copy(x_grouped[i][:, s:w, :].rearrange("p (c i) j -> p c j i", i=4),
+                                          x_raw[load][:, :, a + s:a + w].rearrange("p j (c i) -> p c j i", i=4))
+            for i in pieces:
+                c0, w = sum(X_PIECES[:i]), X_PIECES[i]
+                nc.vector.quantize_mx(out=x_words[:, c0:c0 + w].bitcast(FP8X4), scales=x_bytes[:, c0:c0 + w],
+                                      in_=x_grouped[i][:].rearrange("p c j -> p (c j)"))
 
         cols = CH // 16
 
@@ -107,6 +112,9 @@ def tile_picked_route2_mlprelu_e_kernel(tc, xT, gate, w1, w2_words, w2_scales, o
         gather(gw1_t, x_words, 1)
         gather(gb1_t, x_bytes, 1)
         gw1, gb1 = gw1_t[:], gb1_t[:]
+        gw2 = keep.tile([P, CH], U32, name="gw2", align_bytes=64)
+        gather(gw2, x_words, 2)
+        gb2 = late.tile([P, CH], U8, name="gb2", offset=THIRD_AT, align_bytes=64)
 
         w_words = [keep.tile([P, P], U32, name="w_words%d" % t, align_bytes=64) for t in range(PACK)]
         w_bytes = [keep.tile([P, P], U8, name="w_bytes%d" % t, align_bytes=64) for t in range(PACK)]
@@ -122,14 +130,14 @@ def tile_picked_route2_mlprelu_e_kernel(tc, xT, gate, w1, w2_words, w2_scales, o
                 nc.vector.tensor_copy(w_grouped[u][:, :, m0 + s // 4:m0 + w // 4, :].rearrange("p t m j -> p m j t"),
                                       w_raw[i][:, :, s:w].rearrange("p j (m t) -> p m j t", t=4))
             c0 = c0 + w
+            if c0 == H:
+                gather(gb2, x_bytes, 2)
             if c0 % (H // 2) == 0:
                 for t in range(PACK):
                     nc.vector.quantize_mx(out=w_words[t][:, u * HALF_M:(u + 1) * HALF_M].bitcast(FP8X4),
                                           scales=w_bytes[t][:, u * HALF_M:(u + 1) * HALF_M],
                                           in_=w_grouped[u][:, t, :, :].rearrange("p m j -> p (m j)"))
 
-        gw2 = late.tile([P, CH], U32, name="gw2", offset=RAW_AT, align_bytes=64)
-        gb2 = late.tile([P, CH], U8, name="gb2", offset=RAW_AT + 512, align_bytes=64)
         gw3 = late.tile([P, CH], U32, name="gw3", offset=RAW_AT + 1024, align_bytes=64)
         gb3 = late.tile([P, CH], U8, name="gb3", offset=RAW_AT + 640, align_bytes=64)
         g_words = [gw0, gw1, gw2[:], gw3[:]]
@@ -175,18 +183,16 @@ def tile_picked_route2_mlprelu_e_kernel(tc, xT, gate, w1, w2_words, w2_scales, o
             a, b = sum(groups[:i]), sum(groups[:i + 1])
             nc.vector.tensor_tensor(window[:].indirect(dst_t[:, a * cols:b * cols]), y_tiles[i][:], gate_t[:, a * CH:b * CH], MULT)
 
-        gather(gw2, x_words, 2)
-        gather(gb2, x_bytes, 2)
         gather(gw3, x_words, 3)
         gather(gb3, x_bytes, 3)
         relu_s(0, 0, 4, first(0, 0, 4, "a0"))
-        relu_s(1, 0, 4, first(1, 0, 4, "b"))
+        relu_v(1, 0, 4, first(1, 0, 4, "b"))
         quant(0)
-        relu_v(2, 0, 4, first(2, 0, 4, "c0"))
+        relu_s(2, 0, 4, first(2, 0, 4, "c0"))
+        relu_v(3, 0, 4, first(3, 0, 4, "a1"))
         quant(1)
-        relu_s(3, 0, 4, first(3, 0, 4, "a1"))
-        quant(2)
         empty_s(0, second(0, "y0"))
+        quant(2)
         quant(3)
         scatter(0)
         empty_s(1, second(1, "y1"))
@@ -194,5 +200,4 @@ def tile_picked_route2_mlprelu_e_kernel(tc, xT, gate, w1, w2_words, w2_scales, o
         empty_s(3, second(3, "y3"))
         scatter(1)
 
-        nc.sync.dma_start(out[:, 0:U // 2], window[:, 0:U // 2])
-        nc.scalar.dma_start(out[:, U // 2:U], window[:, U // 2:U])
+        nc.sync.dma_start(out, window[:])

@@ -23,7 +23,7 @@ X_LOADS = [256,256,256,128,128]
 X_PIECES = [256,256,256,128,128]
 X_SCALAR = [160,160,128,128,48]
 W_PIECES = [128,128,128,128]
-W_SCALAR = [128,128,128,40]
+W_SCALAR = [128,128,128,56]
 CH = 128
 HALF_M = P // 2
 RAW_AT = 0
@@ -112,8 +112,6 @@ def tile_picked_route2_mlprelu_e_kernel(tc, xT, gate, w1, w2_words, w2_scales, o
         gather(gw1_t, x_words, 1)
         gather(gb1_t, x_bytes, 1)
         gw1, gb1 = gw1_t[:], gb1_t[:]
-        gw2 = keep.tile([P, CH], U32, name="gw2", align_bytes=64)
-        gather(gw2, x_words, 2)
         gb2 = late.tile([P, CH], U8, name="gb2", offset=THIRD_AT, align_bytes=64)
 
         w_words = [keep.tile([P, P], U32, name="w_words%d" % t, align_bytes=64) for t in range(PACK)]
@@ -138,6 +136,7 @@ def tile_picked_route2_mlprelu_e_kernel(tc, xT, gate, w1, w2_words, w2_scales, o
                                           scales=w_bytes[t][:, u * HALF_M:(u + 1) * HALF_M],
                                           in_=w_grouped[u][:, t, :, :].rearrange("p m j -> p (m j)"))
 
+        gw2 = late.tile([P, CH], U32, name="gw2", offset=RAW_AT, align_bytes=64)
         gw3 = late.tile([P, CH], U32, name="gw3", offset=RAW_AT + 1024, align_bytes=64)
         gb3 = late.tile([P, CH], U8, name="gb3", offset=RAW_AT + 640, align_bytes=64)
         g_words = [gw0, gw1, gw2[:], gw3[:]]
@@ -154,6 +153,13 @@ def tile_picked_route2_mlprelu_e_kernel(tc, xT, gate, w1, w2_words, w2_scales, o
             for t in range(t0, t1):
                 nc.tensor.matmul_mx(out=acc[:, t - t0, :], lhsT=w_words[t][:].bitcast(FP8X4), lhsT_scale=w_bytes[t][:],
                                     rhs=g_words[c].bitcast(FP8X4), rhs_scale=g_bytes[c], start=True, stop=True)
+            return acc
+
+        def first_half(c, n0, tag):
+            acc = psum.tile([P, PACK, CH // 2], F32, name="h_acc%d_half%d" % (c, n0), tag=tag)
+            for t in range(PACK):
+                nc.tensor.matmul_mx(out=acc[:, t, :], lhsT=w_words[t][:].bitcast(FP8X4), lhsT_scale=w_bytes[t][:],
+                                    rhs=g_words[c][:, n0:n0 + CH // 2].bitcast(FP8X4), rhs_scale=g_bytes[c][:, n0:n0 + CH // 2], start=True, stop=True)
             return acc
 
         def relu_s(c, t0, t1, acc):
@@ -183,14 +189,16 @@ def tile_picked_route2_mlprelu_e_kernel(tc, xT, gate, w1, w2_words, w2_scales, o
             a, b = sum(groups[:i]), sum(groups[:i + 1])
             nc.vector.tensor_tensor(window[:].indirect(dst_t[:, a * cols:b * cols]), y_tiles[i][:], gate_t[:, a * CH:b * CH], MULT)
 
+        gather(gw2, x_words, 2)
         gather(gw3, x_words, 3)
         gather(gb3, x_bytes, 3)
         relu_s(0, 0, 4, first(0, 0, 4, "a0"))
         relu_v(1, 0, 4, first(1, 0, 4, "b"))
         quant(0)
         relu_s(2, 0, 4, first(2, 0, 4, "c0"))
-        relu_v(3, 0, 4, first(3, 0, 4, "a1"))
         quant(1)
+        nc.vector.tensor_scalar_max(h_grouped[3][:, 0:CH // 2, :], first_half(3, 0, "a1")[:].rearrange("p t n -> p n t"), 0.0)
+        nc.scalar.activation(h_grouped[3][:, CH // 2:CH, :], first_half(3, CH // 2, "y3")[:].rearrange("p t n -> p n t"), RELU)
         empty_s(0, second(0, "y0"))
         quant(2)
         quant(3)

@@ -208,4 +208,5 @@ def tile_picked_route2_mlprelu_e_kernel(tc, xT, gate, w1, w2_words, w2_scales, o
         empty_s(3, second(3, "y3"))
         scatter(1)
 
-        nc.sync.dma_start(out, window[:])
+        nc.sync.dma_start(out[:, 0:U // 2], window[:, 0:U // 2])
+        nc.scalar.dma_start(out[:, U // 2:U], window[:, U // 2:U])

@@ -19,9 +19,9 @@ MULT = mybir.AluOpType.mult
 
 P = 128
 PACK = 4
-X_LOADS = [256,256,256,128,128]
-X_PIECES = [256,256,256,128,128]
-X_SCALAR = [160,160,128,128,48]
+X_LOADS = [256, 256, 256, 128, 128]
+X_PIECES = [256, 256, 256, 128, 128]
+X_SCALAR = [160, 160, 128, 128, 48]
 W_PIECES = [128,128,128,128]
 W_SCALAR = [128,128,128,56]
 CH = 128
@@ -95,18 +95,15 @@ def tile_picked_route2_mlprelu_e_kernel(tc, xT, gate, w1, w2_words, w2_scales, o
         def gather(tile, source, c):
             nc.vector.tensor_copy(tile[:], source[:].indirect(offs_t[:, c * cols:(c + 1) * cols]))
 
-        gw_wide = keep.tile([P, 4 * CH], I32, name="gw_early", align_bytes=64)
-        gb_early = keep.tile([P, 4 * CH], U8, name="gb_early", align_bytes=64)
-        nc.vector.memset(gw_wide[:, CH:4 * CH], 0)
-        nc.vector.memset(gb_early[:, CH:4 * CH].bitcast(I32), 0)
-        gw_early = gw_wide[:].bitcast(U32)
-        gw0, gb0 = gw_early[:, 0:CH], gb_early[:, 0:CH]
-        nc.vector.tensor_copy(gw0, x_words[:].indirect(offs_t[:, 0:cols]))
-        nc.vector.tensor_copy(gb0, x_bytes[:].indirect(offs_t[:, 0:cols]))
-        for u in range(2):
-            warm = psum.tile([32, 4 * CH], F32, name="warm%d" % u, tag="y%d" % (2 + u))
-            nc.tensor.matmul_mx(out=warm[:], lhsT=gw_early[:, 0:32].bitcast(FP8X4), lhsT_scale=gb_early[:, 0:32],
-                                rhs=gw_early.bitcast(FP8X4), rhs_scale=gb_early[:], start=True, stop=True)
+        gw0_t = keep.tile([P, CH], U32, name="gw0", align_bytes=64)
+        gb0_t = keep.tile([P, CH], U8, name="gb0", align_bytes=64)
+        gather(gw0_t, x_words, 0)
+        gather(gb0_t, x_bytes, 0)
+        gw0, gb0 = gw0_t[:], gb0_t[:]
+        warm = psum.tile([32, PACK, CH], F32, name="warm", tag="y2")
+        for u in range(8):
+            nc.tensor.matmul_mx(out=warm[:, u % PACK, :], lhsT=gw0[:, 0:32].bitcast(FP8X4), lhsT_scale=gb0[:, 0:32],
+                                rhs=gw0.bitcast(FP8X4), rhs_scale=gb0, start=True, stop=True)
         gw1_t = keep.tile([P, CH], U32, name="gw1", align_bytes=64)
         gb1_t = keep.tile([P, CH], U8, name="gb1", align_bytes=64)
         gather(gw1_t, x_words, 1)

@@ -52,10 +52,14 @@ def tile_picked_route2_mlprelu_e_kernel(tc, xT, gate, w1, w2_words, w2_scales, o
 
         nc.vector.memset(x_bytes[:].bitcast(I32), 0)
         nc.vector.memset(window[:], 0.0)
+        w_bytes_t = keep.tile([P, PACK, P], U8, name="w_bytes", align_bytes=64)
+        nc.vector.memset(w_bytes_t[:].bitcast(I32), 0)
 
         x_view = xT.rearrange("(p j) t -> p j t", j=PACK)
         w_view = w1.rearrange("(p j) c -> p j c", j=PACK)
-        x_raw = [keep.tile([P, PACK, w], F32, name="x_raw%d" % i) for i, w in enumerate(X_LOADS)]
+        x_raw = [keep.tile([P, PACK, w], F32, name="x_raw%d" % i) for i, w in enumerate(X_LOADS[:3])]
+        x_raw.append(late.tile([P, PACK, X_LOADS[3]], F32, name="x_raw3", offset=G_AT, align_bytes=64))
+        x_raw.append(keep.tile([P, PACK, X_LOADS[4]], F32, name="x_raw4"))
         w_raw = [keep.tile([P, PACK, w], F32, name="w_raw%d" % i) for i, w in enumerate(W_PIECES[:-2])]
         w_raw.append(late.tile([P, PACK, W_PIECES[-2]], F32, name="w_raw_third", offset=THIRD_AT, align_bytes=64))
         w_raw.append(late.tile([P, PACK, W_PIECES[-1]], F32, name="w_raw_last", offset=RAW_AT, align_bytes=64))
@@ -65,14 +69,38 @@ def tile_picked_route2_mlprelu_e_kernel(tc, xT, gate, w1, w2_words, w2_scales, o
             for q in range(4):
                 queue.dma_start(w2_plane[32 * q:32 * q + 4, :].bitcast(I32), w2_scales[0, 4 * q:4 * q + 4, :].bitcast(I32))
 
+        nc.sync.dma_start(w_raw[0][:], w_view[:, :, 0:W_PIECES[0]])
         for i in range(len(X_LOADS)):
             nc.sync.dma_start(x_raw[i][:], x_view[:, :, sum(X_LOADS[:i]):sum(X_LOADS[:i + 1])])
         nc.sync.dma_start(offs_t[:], offs)
-        for i in range(len(W_PIECES)):
+        for i in range(1, len(W_PIECES)):
             nc.sync.dma_start(w_raw[i][:], w_view[:, :, sum(W_PIECES[:i]):sum(W_PIECES[:i + 1])])
         load_w2(nc.sync)
         nc.sync.dma_start(dst_t[:], dst)
         nc.sync.dma_start(gate_t[:], gate)
+
+        w_words_t = keep.tile([P, PACK, P], U32, name="w_words", align_bytes=64)
+        w_words = [w_words_t[:, t, :] for t in range(PACK)]
+        w_bytes = [w_bytes_t[:, t, :] for t in range(PACK)]
+        w_grouped = [keep.tile([P, PACK, HALF_M, PACK], BF16, name="w_grouped%d" % u, align_bytes=64) for u in range(2)]
+
+        def round_w(i):
+            s, w = W_SCALAR[i], W_PIECES[i]
+            u, m0 = divmod(sum(W_PIECES[:i]) // PACK, HALF_M)
+            nc.scalar.activation(w_grouped[u][:, :, m0:m0 + s // 4, :].rearrange("p t m j -> p m j t"),
+                                 w_raw[i][:, :, 0:s].rearrange("p j (m t) -> p m j t", t=4), COPY)
+            if s < w:
+                nc.vector.tensor_copy(w_grouped[u][:, :, m0 + s // 4:m0 + w // 4, :].rearrange("p t m j -> p m j t"),
+                                      w_raw[i][:, :, s:w].rearrange("p j (m t) -> p m j t", t=4))
+
+        def quant_w(a, b):
+            u, m0 = divmod(a, HALF_M)
+            for t in range(PACK):
+                nc.vector.quantize_mx(out=w_words[t][:, a:b].bitcast(FP8X4), scales=w_bytes[t][:, a:b],
+                                      in_=w_grouped[u][:, t, m0:m0 + b - a, :].rearrange("p m j -> p (m j)"))
+
+        round_w(0)
+        quant_w(0, 32)
 
         x_grouped = [keep.tile([P, w, PACK], BF16, name="x_grouped%d" % i, align_bytes=64) for i, w in enumerate(X_PIECES)]
         for load in range(len(X_LOADS)):
@@ -90,6 +118,16 @@ def tile_picked_route2_mlprelu_e_kernel(tc, xT, gate, w1, w2_words, w2_scales, o
                 nc.vector.quantize_mx(out=x_words[:, c0:c0 + w].bitcast(FP8X4), scales=x_bytes[:, c0:c0 + w],
                                       in_=x_grouped[i][:].rearrange("p c j -> p (c j)"))
 
+        warm_words = keep.tile([P, PACK, PACK, 32], I32, name="warm_words", align_bytes=64)
+        warm_bytes = late.tile([P, PACK, PACK, 32], U8, name="warm_bytes", offset=G_AT, align_bytes=64)
+        nc.vector.tensor_copy(warm_bytes[:].bitcast(I32), w_bytes_t[:, :, 0:32].bitcast(I32).unsqueeze(1).to_broadcast([P, PACK, PACK, 8]))
+        nc.vector.tensor_copy(warm_words[:], w_words_t[:, :, 0:32].bitcast(I32).unsqueeze(1).to_broadcast([P, PACK, PACK, 32]))
+        for u in range(2):
+            warm = psum.tile([32, PACK * CH], F32, name="warm%d" % u, tag="y%d" % (2 + u))
+            nc.tensor.matmul_mx(out=warm[:], lhsT=w_words[0][:, 0:32].bitcast(FP8X4), lhsT_scale=w_bytes[0][:, 0:32],
+                                rhs=warm_words[:].rearrange("p r t n -> p (r t n)").bitcast(FP8X4),
+                                rhs_scale=warm_bytes[:].rearrange("p r t n -> p (r t n)"), start=True, stop=True)
+
         cols = CH // 16
 
         def gather(tile, source, c):
@@ -100,38 +138,18 @@ def tile_picked_route2_mlprelu_e_kernel(tc, xT, gate, w1, w2_words, w2_scales, o
         gather(gw0_t, x_words, 0)
         gather(gb0_t, x_bytes, 0)
         gw0, gb0 = gw0_t[:], gb0_t[:]
-        warm = psum.tile([32, PACK, CH], F32, name="warm", tag="y2")
-        for u in range(8):
-            nc.tensor.matmul_mx(out=warm[:, u % PACK, :], lhsT=gw0[:, 0:32].bitcast(FP8X4), lhsT_scale=gb0[:, 0:32],
-                                rhs=gw0.bitcast(FP8X4), rhs_scale=gb0, start=True, stop=True)
         gw1_t = keep.tile([P, CH], U32, name="gw1", align_bytes=64)
-        gb1_t = keep.tile([P, CH], U8, name="gb1", align_bytes=64)
-        gather(gw1_t, x_words, 1)
-        gather(gb1_t, x_bytes, 1)
+        gb1_t = late.tile([P, CH], U8, name="gb1", offset=THIRD_AT, align_bytes=64)
         gw1, gb1 = gw1_t[:], gb1_t[:]
-        gb2 = late.tile([P, CH], U8, name="gb2", offset=THIRD_AT, align_bytes=64)
 
-        w_words = [keep.tile([P, P], U32, name="w_words%d" % t, align_bytes=64) for t in range(PACK)]
-        w_bytes = [keep.tile([P, P], U8, name="w_bytes%d" % t, align_bytes=64) for t in range(PACK)]
-        w_grouped = [keep.tile([P, PACK, HALF_M, PACK], BF16, name="w_grouped%d" % u, align_bytes=64) for u in range(2)]
-        c0 = 0
-        for i, w in enumerate(W_PIECES):
-            s = W_SCALAR[i]
-            u, m0 = divmod(c0 // PACK, HALF_M)
-            if s > 0:
-                nc.scalar.activation(w_grouped[u][:, :, m0:m0 + s // 4, :].rearrange("p t m j -> p m j t"),
-                                     w_raw[i][:, :, 0:s].rearrange("p j (m t) -> p m j t", t=4), COPY)
-            if s < w:
-                nc.vector.tensor_copy(w_grouped[u][:, :, m0 + s // 4:m0 + w // 4, :].rearrange("p t m j -> p m j t"),
-                                      w_raw[i][:, :, s:w].rearrange("p j (m t) -> p m j t", t=4))
-            c0 = c0 + w
-            if c0 == H:
-                gather(gb2, x_bytes, 2)
-            if c0 % (H // 2) == 0:
-                for t in range(PACK):
-                    nc.vector.quantize_mx(out=w_words[t][:, u * HALF_M:(u + 1) * HALF_M].bitcast(FP8X4),
-                                          scales=w_bytes[t][:, u * HALF_M:(u + 1) * HALF_M],
-                                          in_=w_grouped[u][:, t, :, :].rearrange("p m j -> p (m j)"))
+        round_w(1)
+        gather(gw1_t, x_words, 1)
+        quant_w(32, 64)
+        round_w(2)
+        round_w(3)
+        gather(gb1_t, x_bytes, 1)
+        quant_w(64, 128)
+        gb2 = late.tile([P, CH], U8, name="gb2", offset=RAW_AT + 768, align_bytes=64)
 
         gw2 = late.tile([P, CH], U32, name="gw2", offset=RAW_AT, align_bytes=64)
         gw3 = late.tile([P, CH], U32, name="gw3", offset=RAW_AT + 1024, align_bytes=64)
@@ -148,14 +166,14 @@ def tile_picked_route2_mlprelu_e_kernel(tc, xT, gate, w1, w2_words, w2_scales, o
         def first(c, t0, t1, tag):
             acc = psum.tile([P, t1 - t0, CH], F32, name="h_acc%d_%d" % (c, t0), tag=tag)
             for t in range(t0, t1):
-                nc.tensor.matmul_mx(out=acc[:, t - t0, :], lhsT=w_words[t][:].bitcast(FP8X4), lhsT_scale=w_bytes[t][:],
+                nc.tensor.matmul_mx(out=acc[:, t - t0, :], lhsT=w_words[t].bitcast(FP8X4), lhsT_scale=w_bytes[t],
                                     rhs=g_words[c].bitcast(FP8X4), rhs_scale=g_bytes[c], start=True, stop=True)
             return acc
 
         def first_half(c, n0, tag):
             acc = psum.tile([P, PACK, CH // 2], F32, name="h_acc%d_half%d" % (c, n0), tag=tag)
             for t in range(PACK):
-                nc.tensor.matmul_mx(out=acc[:, t, :], lhsT=w_words[t][:].bitcast(FP8X4), lhsT_scale=w_bytes[t][:],
+                nc.tensor.matmul_mx(out=acc[:, t, :], lhsT=w_words[t].bitcast(FP8X4), lhsT_scale=w_bytes[t],
                                     rhs=g_words[c][:, n0:n0 + CH // 2].bitcast(FP8X4), rhs_scale=g_bytes[c][:, n0:n0 + CH // 2], start=True, stop=True)
             return acc
 
@@ -187,6 +205,7 @@ def tile_picked_route2_mlprelu_e_kernel(tc, xT, gate, w1, w2_words, w2_scales, o
             nc.vector.tensor_tensor(window[:].indirect(dst_t[:, a * cols:b * cols]), y_tiles[i][:], gate_t[:, a * CH:b * CH], MULT)
 
         gather(gw2, x_words, 2)
+        gather(gb2, x_bytes, 2)
         gather(gw3, x_words, 3)
         gather(gb3, x_bytes, 3)
         relu_s(0, 0, 4, first(0, 0, 4, "a0"))

@@ -52,14 +52,10 @@ def tile_picked_route2_mlprelu_e_kernel(tc, xT, gate, w1, w2_words, w2_scales, o
 
         nc.vector.memset(x_bytes[:].bitcast(I32), 0)
         nc.vector.memset(window[:], 0.0)
-        w_bytes_t = keep.tile([P, PACK, P], U8, name="w_bytes", align_bytes=64)
-        nc.vector.memset(w_bytes_t[:].bitcast(I32), 0)
 
         x_view = xT.rearrange("(p j) t -> p j t", j=PACK)
         w_view = w1.rearrange("(p j) c -> p j c", j=PACK)
-        x_raw = [keep.tile([P, PACK, w], F32, name="x_raw%d" % i) for i, w in enumerate(X_LOADS[:3])]
-        x_raw.append(late.tile([P, PACK, X_LOADS[3]], F32, name="x_raw3", offset=G_AT, align_bytes=64))
-        x_raw.append(keep.tile([P, PACK, X_LOADS[4]], F32, name="x_raw4"))
+        x_raw = [keep.tile([P, PACK, w], F32, name="x_raw%d" % i) for i, w in enumerate(X_LOADS)]
         w_raw = [keep.tile([P, PACK, w], F32, name="w_raw%d" % i) for i, w in enumerate(W_PIECES[:-2])]
         w_raw.append(late.tile([P, PACK, W_PIECES[-2]], F32, name="w_raw_third", offset=THIRD_AT, align_bytes=64))
         w_raw.append(late.tile([P, PACK, W_PIECES[-1]], F32, name="w_raw_last", offset=RAW_AT, align_bytes=64))
@@ -79,28 +75,34 @@ def tile_picked_route2_mlprelu_e_kernel(tc, xT, gate, w1, w2_words, w2_scales, o
         nc.sync.dma_start(dst_t[:], dst)
         nc.sync.dma_start(gate_t[:], gate)
 
-        w_words_t = keep.tile([P, PACK, P], U32, name="w_words", align_bytes=64)
-        w_words = [w_words_t[:, t, :] for t in range(PACK)]
-        w_bytes = [w_bytes_t[:, t, :] for t in range(PACK)]
-        w_grouped = [keep.tile([P, PACK, HALF_M, PACK], BF16, name="w_grouped%d" % u, align_bytes=64) for u in range(2)]
+        w_words = [keep.tile([P, P], U32, name="w_words%d" % t, align_bytes=64)[:] for t in range(PACK)]
+        w_bytes = [keep.tile([P, P], U8, name="w_bytes%d" % t, align_bytes=64)[:] for t in range(PACK)]
+        spans = [(0, 32), (32, 64), (64, 128)]
+        w_grouped = [keep.tile([P, PACK, b - a, PACK], BF16, name="w_grouped%d" % a, align_bytes=64) for a, b in spans]
 
         def round_w(i):
             s, w = W_SCALAR[i], W_PIECES[i]
-            u, m0 = divmod(sum(W_PIECES[:i]) // PACK, HALF_M)
+            u = min(i, 2)
+            m0 = sum(W_PIECES[:i]) // PACK - spans[u][0]
             nc.scalar.activation(w_grouped[u][:, :, m0:m0 + s // 4, :].rearrange("p t m j -> p m j t"),
                                  w_raw[i][:, :, 0:s].rearrange("p j (m t) -> p m j t", t=4), COPY)
             if s < w:
                 nc.vector.tensor_copy(w_grouped[u][:, :, m0 + s // 4:m0 + w // 4, :].rearrange("p t m j -> p m j t"),
                                       w_raw[i][:, :, s:w].rearrange("p j (m t) -> p m j t", t=4))
 
-        def quant_w(a, b):
-            u, m0 = divmod(a, HALF_M)
+        def quant_w(u):
+            a, b = spans[u]
             for t in range(PACK):
                 nc.vector.quantize_mx(out=w_words[t][:, a:b].bitcast(FP8X4), scales=w_bytes[t][:, a:b],
-                                      in_=w_grouped[u][:, t, m0:m0 + b - a, :].rearrange("p m j -> p (m j)"))
+                                      in_=w_grouped[u][:, t, :, :].rearrange("p m j -> p (m j)"))
 
         round_w(0)
-        quant_w(0, 32)
+        warm_words = keep.tile([P, PACK * CH], U32, name="warm_words", align_bytes=64)
+        warm_bytes = keep.tile([P, PACK * CH], U8, name="warm_bytes", align_bytes=64)
+        for r in range(PACK):
+            nc.vector.quantize_mx(out=warm_words[:, r * CH:(r + 1) * CH].bitcast(FP8X4), scales=warm_bytes[:, r * CH:(r + 1) * CH],
+                                  in_=w_grouped[0][:].rearrange("p t m j -> p (t m j)"))
+        quant_w(0)
 
         x_grouped = [keep.tile([P, w, PACK], BF16, name="x_grouped%d" % i, align_bytes=64) for i, w in enumerate(X_PIECES)]
         for load in range(len(X_LOADS)):
@@ -118,16 +120,6 @@ def tile_picked_route2_mlprelu_e_kernel(tc, xT, gate, w1, w2_words, w2_scales, o
                 nc.vector.quantize_mx(out=x_words[:, c0:c0 + w].bitcast(FP8X4), scales=x_bytes[:, c0:c0 + w],
                                       in_=x_grouped[i][:].rearrange("p c j -> p (c j)"))
 
-        warm_words = keep.tile([P, PACK, PACK, 32], I32, name="warm_words", align_bytes=64)
-        warm_bytes = late.tile([P, PACK, PACK, 32], U8, name="warm_bytes", offset=G_AT, align_bytes=64)
-        nc.vector.tensor_copy(warm_bytes[:].bitcast(I32), w_bytes_t[:, :, 0:32].bitcast(I32).unsqueeze(1).to_broadcast([P, PACK, PACK, 8]))
-        nc.vector.tensor_copy(warm_words[:], w_words_t[:, :, 0:32].bitcast(I32).unsqueeze(1).to_broadcast([P, PACK, PACK, 32]))
-        for u in range(2):
-            warm = psum.tile([32, PACK * CH], F32, name="warm%d" % u, tag="y%d" % (2 + u))
-            nc.tensor.matmul_mx(out=warm[:], lhsT=w_words[0][:, 0:32].bitcast(FP8X4), lhsT_scale=w_bytes[0][:, 0:32],
-                                rhs=warm_words[:].rearrange("p r t n -> p (r t n)").bitcast(FP8X4),
-                                rhs_scale=warm_bytes[:].rearrange("p r t n -> p (r t n)"), start=True, stop=True)
-
         cols = CH // 16
 
         def gather(tile, source, c):
@@ -138,17 +130,21 @@ def tile_picked_route2_mlprelu_e_kernel(tc, xT, gate, w1, w2_words, w2_scales, o
         gather(gw0_t, x_words, 0)
         gather(gb0_t, x_bytes, 0)
         gw0, gb0 = gw0_t[:], gb0_t[:]
+        for u in range(2):
+            warm = psum.tile([32, PACK * CH], F32, name="warm%d" % u, tag="y%d" % (2 + u))
+            nc.tensor.matmul_mx(out=warm[:], lhsT=gw0[:, 0:32].bitcast(FP8X4), lhsT_scale=warm_bytes[:, 0:32],
+                                rhs=warm_words[:].bitcast(FP8X4), rhs_scale=warm_bytes[:], start=True, stop=True)
         gw1_t = keep.tile([P, CH], U32, name="gw1", align_bytes=64)
         gb1_t = late.tile([P, CH], U8, name="gb1", offset=THIRD_AT, align_bytes=64)
         gw1, gb1 = gw1_t[:], gb1_t[:]
 
         round_w(1)
         gather(gw1_t, x_words, 1)
-        quant_w(32, 64)
+        quant_w(1)
         round_w(2)
         round_w(3)
         gather(gb1_t, x_bytes, 1)
-        quant_w(64, 128)
+        quant_w(2)
         gb2 = late.tile([P, CH], U8, name="gb2", offset=RAW_AT + 768, align_bytes=64)
 
         gw2 = late.tile([P, CH], U32, name="gw2", offset=RAW_AT, align_bytes=64)

@@ -23,7 +23,7 @@ X_LOADS = [256, 256, 256, 128, 128]
 X_PIECES = [256, 256, 256, 128, 128]
 X_SCALAR = [160, 160, 128, 128, 48]
 W_PIECES = [128,128,128,128]
-W_SCALAR = [128,128,128,56]
+W_SCALAR = [128,128,128,104]
 CH = 128
 HALF_M = P // 2
 RAW_AT = 0
@@ -135,17 +135,18 @@ def tile_picked_route2_mlprelu_e_kernel(tc, xT, gate, w1, w2_words, w2_scales, o
             nc.tensor.matmul_mx(out=warm[:], lhsT=gw0[:, 0:32].bitcast(FP8X4), lhsT_scale=warm_bytes[:, 0:32],
                                 rhs=warm_words[:].bitcast(FP8X4), rhs_scale=warm_bytes[:], start=True, stop=True)
         gw1_t = keep.tile([P, CH], U32, name="gw1", align_bytes=64)
-        gb1_t = late.tile([P, CH], U8, name="gb1", offset=THIRD_AT, align_bytes=64)
+        gb1_t = keep.tile([P, CH], U8, name="gb1", align_bytes=64)
         gw1, gb1 = gw1_t[:], gb1_t[:]
 
         round_w(1)
         gather(gw1_t, x_words, 1)
         quant_w(1)
+        gather(gb1_t, x_bytes, 1)
         round_w(2)
         round_w(3)
-        gather(gb1_t, x_bytes, 1)
+        gb2 = late.tile([P, CH], U8, name="gb2", offset=THIRD_AT, align_bytes=64)
+        gather(gb2, x_bytes, 2)
         quant_w(2)
-        gb2 = late.tile([P, CH], U8, name="gb2", offset=RAW_AT + 768, align_bytes=64)
 
         gw2 = late.tile([P, CH], U32, name="gw2", offset=RAW_AT, align_bytes=64)
         gw3 = late.tile([P, CH], U32, name="gw3", offset=RAW_AT + 1024, align_bytes=64)
@@ -164,13 +165,6 @@ def tile_picked_route2_mlprelu_e_kernel(tc, xT, gate, w1, w2_words, w2_scales, o
             for t in range(t0, t1):
                 nc.tensor.matmul_mx(out=acc[:, t - t0, :], lhsT=w_words[t].bitcast(FP8X4), lhsT_scale=w_bytes[t],
                                     rhs=g_words[c].bitcast(FP8X4), rhs_scale=g_bytes[c], start=True, stop=True)
-            return acc
-
-        def first_half(c, n0, tag):
-            acc = psum.tile([P, PACK, CH // 2], F32, name="h_acc%d_half%d" % (c, n0), tag=tag)
-            for t in range(PACK):
-                nc.tensor.matmul_mx(out=acc[:, t, :], lhsT=w_words[t].bitcast(FP8X4), lhsT_scale=w_bytes[t],
-                                    rhs=g_words[c][:, n0:n0 + CH // 2].bitcast(FP8X4), rhs_scale=g_bytes[c][:, n0:n0 + CH // 2], start=True, stop=True)
             return acc
 
         def relu_s(c, t0, t1, acc):
@@ -201,7 +195,6 @@ def tile_picked_route2_mlprelu_e_kernel(tc, xT, gate, w1, w2_words, w2_scales, o
             nc.vector.tensor_tensor(window[:].indirect(dst_t[:, a * cols:b * cols]), y_tiles[i][:], gate_t[:, a * CH:b * CH], MULT)
 
         gather(gw2, x_words, 2)
-        gather(gb2, x_bytes, 2)
         gather(gw3, x_words, 3)
         gather(gb3, x_bytes, 3)
         relu_s(0, 0, 4, first(0, 0, 4, "a0"))
@@ -209,8 +202,8 @@ def tile_picked_route2_mlprelu_e_kernel(tc, xT, gate, w1, w2_words, w2_scales, o
         quant(0)
         relu_s(2, 0, 4, first(2, 0, 4, "c0"))
         quant(1)
-        nc.vector.tensor_scalar_max(h_grouped[3][:, 0:CH // 2, :], first_half(3, 0, "a1")[:].rearrange("p t n -> p n t"), 0.0)
-        nc.scalar.activation(h_grouped[3][:, CH // 2:CH, :], first_half(3, CH // 2, "y3")[:].rearrange("p t n -> p n t"), RELU)
+        relu_v(3, 0, 2, first(3, 0, 2, "a1"))
+        relu_s(3, 2, 4, first(3, 2, 4, "y3"))
         empty_s(0, second(0, "y0"))
         quant(2)
         quant(3)

@@ -19,18 +19,9 @@ MULT = mybir.AluOpType.mult
 
 P = 128
 PACK = 4
-X_LOADS = [256, 256, 256, 128, 128]
-X_PIECES = [256, 256, 256, 128, 128]
-X_SCALAR = [160, 160, 128, 128, 48]
-W_PIECES = [128,128,128,128]
-W_SCALAR = [128,128,128,104]
 CH = 128
-HALF_M = P // 2
-RAW_AT = 0
-THIRD_AT = 2048
-G_AT = 8192
-H0_AT = 12288
-Q_AT = 16384
+W_VECTOR = 88
+WARM_M = 32
 
 
 def tile_picked_route2_mlprelu_e_kernel(tc, xT, gate, w1, w2_words, w2_scales, offs, dst, out):
@@ -42,129 +33,103 @@ def tile_picked_route2_mlprelu_e_kernel(tc, xT, gate, w1, w2_words, w2_scales, o
 
         offs_t = keep.tile([P, S // 16], U16, name="offs_t")
         dst_t = keep.tile([P, S // 16], U16, name="dst_t")
-        x_words = keep.tile([P, T], U32, name="x_words", align_bytes=64)
-        x_bytes = keep.tile([P, T], U8, name="x_bytes", align_bytes=64)
         w2_codes = keep.tile([P, 2 * N], U8, name="w2_codes", align_bytes=64)
         w2_plane = keep.tile([P, N], U8, name="w2_plane", align_bytes=64)
         gate_t = keep.tile([P, S], F32, name="gate_t")
         window = keep.tile([P, U], F32, name="window")
-
-
-        nc.vector.memset(x_bytes[:].bitcast(I32), 0)
         nc.vector.memset(window[:], 0.0)
 
         x_view = xT.rearrange("(p j) t -> p j t", j=PACK)
-        w_view = w1.rearrange("(p j) c -> p j c", j=PACK)
-        x_raw = [keep.tile([P, PACK, w], F32, name="x_raw%d" % i) for i, w in enumerate(X_LOADS)]
-        w_raw = [keep.tile([P, PACK, w], F32, name="w_raw%d" % i) for i, w in enumerate(W_PIECES[:-2])]
-        w_raw.append(late.tile([P, PACK, W_PIECES[-2]], F32, name="w_raw_third", offset=THIRD_AT, align_bytes=64))
-        w_raw.append(late.tile([P, PACK, W_PIECES[-1]], F32, name="w_raw_last", offset=RAW_AT, align_bytes=64))
+        w_raw = keep.tile([P, PACK, H], F32, name="w_raw")
+        planes = [late.tile([P, T], F32, name="plane%d" % j, offset=4 * T * j, align_bytes=64) for j in range(PACK)]
 
-        def load_w2(queue):
-            queue.dma_start(w2_codes[:].bitcast(I32), w2_words[0].bitcast(I32))
-            for q in range(4):
-                queue.dma_start(w2_plane[32 * q:32 * q + 4, :].bitcast(I32), w2_scales[0, 4 * q:4 * q + 4, :].bitcast(I32))
-
-        nc.sync.dma_start(w_raw[0][:], w_view[:, :, 0:W_PIECES[0]])
-        for i in range(len(X_LOADS)):
-            nc.sync.dma_start(x_raw[i][:], x_view[:, :, sum(X_LOADS[:i]):sum(X_LOADS[:i + 1])])
+        nc.sync.dma_start(w_raw[:], w1.rearrange("(p j) c -> p j c", j=PACK))
         nc.sync.dma_start(offs_t[:], offs)
-        for i in range(1, len(W_PIECES)):
-            nc.sync.dma_start(w_raw[i][:], w_view[:, :, sum(W_PIECES[:i]):sum(W_PIECES[:i + 1])])
-        load_w2(nc.sync)
+        for j in range(PACK):
+            nc.sync.dma_start(planes[j][:], x_view[:, j, :])
+        nc.sync.dma_start(w2_codes[:].bitcast(I32), w2_words[0].bitcast(I32))
+        for q in range(4):
+            nc.sync.dma_start(w2_plane[32 * q:32 * q + 4, :].bitcast(I32), w2_scales[0, 4 * q:4 * q + 4, :].bitcast(I32))
         nc.sync.dma_start(dst_t[:], dst)
         nc.sync.dma_start(gate_t[:], gate)
 
-        w_words = [keep.tile([P, P], U32, name="w_words%d" % t, align_bytes=64)[:] for t in range(PACK)]
-        w_bytes = [keep.tile([P, P], U8, name="w_bytes%d" % t, align_bytes=64)[:] for t in range(PACK)]
-        spans = [(0, 32), (32, 64), (64, 128)]
-        w_grouped = [keep.tile([P, PACK, b - a, PACK], BF16, name="w_grouped%d" % a, align_bytes=64) for a, b in spans]
+        w_grouped = keep.tile([P, PACK, P, PACK], BF16, name="w_grouped", align_bytes=64)
+        w_words = keep.tile([P, H], U32, name="w_words", align_bytes=64)
+        w_bytes = keep.tile([P, H], U8, name="w_bytes", align_bytes=64)
 
-        def round_w(i):
-            s, w = W_SCALAR[i], W_PIECES[i]
-            u = min(i, 2)
-            m0 = sum(W_PIECES[:i]) // PACK - spans[u][0]
-            nc.scalar.activation(w_grouped[u][:, :, m0:m0 + s // 4, :].rearrange("p t m j -> p m j t"),
-                                 w_raw[i][:, :, 0:s].rearrange("p j (m t) -> p m j t", t=4), COPY)
-            if s < w:
-                nc.vector.tensor_copy(w_grouped[u][:, :, m0 + s // 4:m0 + w // 4, :].rearrange("p t m j -> p m j t"),
-                                      w_raw[i][:, :, s:w].rearrange("p j (m t) -> p m j t", t=4))
+        def w_views(a, b):
+            return (w_grouped[:, :, a:b, :].rearrange("p t m j -> p m j t"),
+                    w_raw[:, :, PACK * a:PACK * b].rearrange("p j (m t) -> p m j t", t=PACK))
 
-        def quant_w(u):
-            a, b = spans[u]
-            for t in range(PACK):
-                nc.vector.quantize_mx(out=w_words[t][:, a:b].bitcast(FP8X4), scales=w_bytes[t][:, a:b],
-                                      in_=w_grouped[u][:, t, :, :].rearrange("p m j -> p (m j)"))
+        nc.vector.tensor_copy(*w_views(0, W_VECTOR))
+        nc.scalar.activation(*w_views(W_VECTOR, P), COPY)
+        nc.vector.quantize_mx(out=w_words[:].bitcast(FP8X4), scales=w_bytes[:], in_=w_grouped[:].rearrange("p t m j -> p (t m j)"))
 
-        round_w(0)
-        warm_words = keep.tile([P, PACK * CH], U32, name="warm_words", align_bytes=64)
-        warm_bytes = keep.tile([P, PACK * CH], U8, name="warm_bytes", align_bytes=64)
-        for r in range(PACK):
-            nc.vector.quantize_mx(out=warm_words[:, r * CH:(r + 1) * CH].bitcast(FP8X4), scales=warm_bytes[:, r * CH:(r + 1) * CH],
-                                  in_=w_grouped[0][:].rearrange("p t m j -> p (t m j)"))
-        quant_w(0)
+        low = keep.tile([P, 2, S], BF16, name="low")
+        high = [keep.tile([P, 2, CH], BF16, name="high%d" % c) for c in range(4)]
+        x_grouped = [keep.tile([P, CH, PACK], BF16, name="x_grouped%d" % c, align_bytes=64) for c in range(4)]
+        g_words = [keep.tile([P, CH], U32, name="g_words%d" % c, align_bytes=64) for c in range(4)]
+        g_bytes = [keep.tile([P, CH], U8, name="g_bytes%d" % c, align_bytes=64) for c in range(4)]
 
-        x_grouped = [keep.tile([P, w, PACK], BF16, name="x_grouped%d" % i, align_bytes=64) for i, w in enumerate(X_PIECES)]
-        for load in range(len(X_LOADS)):
-            first_token = sum(X_LOADS[:load])
-            pieces = [i for i in range(len(X_PIECES)) if first_token <= sum(X_PIECES[:i]) < first_token + X_LOADS[load]]
-            for i in pieces:
-                a, s, w = sum(X_PIECES[:i]) - first_token, X_SCALAR[i], X_PIECES[i]
-                nc.scalar.activation(x_grouped[i][:, 0:s, :].rearrange("p (c i) j -> p c j i", i=4),
-                                     x_raw[load][:, :, a:a + s].rearrange("p j (c i) -> p c j i", i=4), COPY)
-                if s < w:
-                    nc.vector.tensor_copy(x_grouped[i][:, s:w, :].rearrange("p (c i) j -> p c j i", i=4),
-                                          x_raw[load][:, :, a + s:a + w].rearrange("p j (c i) -> p c j i", i=4))
-            for i in pieces:
-                c0, w = sum(X_PIECES[:i]), X_PIECES[i]
-                nc.vector.quantize_mx(out=x_words[:, c0:c0 + w].bitcast(FP8X4), scales=x_bytes[:, c0:c0 + w],
-                                      in_=x_grouped[i][:].rearrange("p c j -> p (c j)"))
+        def gather_v(target, j, a, b):
+            nc.vector.tensor_copy(target, planes[j][:].indirect(offs_t[:, a // 16:b // 16]))
+
+        def gather_s(target, j, a, b):
+            nc.scalar.activation(target, planes[j][:].indirect(offs_t[:, a // 16:b // 16]), COPY)
+
+        def weave_views(c, t0, source):
+            return (x_grouped[c][:, :, t0:t0 + 2].rearrange("p (n i) t -> p n t i", i=4),
+                    source.rearrange("p t (n i) -> p n t i", i=4))
+
+        def quant_x(c):
+            nc.vector.quantize_mx(out=g_words[c][:].bitcast(FP8X4), scales=g_bytes[c][:], in_=x_grouped[c][:].rearrange("p n t -> p (n t)"))
+
+        gather_s(low[:, 0, :], 0, 0, S)
+        gather_v(low[:, 1, 0:S // 2], 1, 0, S // 2)
+        gather_s(low[:, 1, S // 2:S], 1, S // 2, S)
+
+        warm_words = late.tile([P, WARM_M], U32, name="warm_words", offset=4 * T, align_bytes=64)
+        warm_bytes = keep.tile([P, WARM_M], U8, name="warm_bytes", align_bytes=64)
+        nc.vector.quantize_mx(out=warm_words[:].bitcast(FP8X4), scales=warm_bytes[:],
+                              in_=w_grouped[:, 0, 0:WARM_M, :].rearrange("p m j -> p (m j)"))
+        for u in range(2):
+            warm = psum.tile([WARM_M, H], F32, name="warm%d" % u, tag="y%d" % (2 + u))
+            nc.tensor.matmul_mx(out=warm[:], lhsT=warm_words[:].bitcast(FP8X4), lhsT_scale=warm_bytes[:],
+                                rhs=w_words[:].bitcast(FP8X4), rhs_scale=w_bytes[:], start=True, stop=True)
+
+        for c in range(4):
+            nc.vector.tensor_copy(*weave_views(c, 0, low[:, :, c * CH:(c + 1) * CH]))
+        for c in (0, 2, 3):
+            gather_s(high[c][:, 0, :], 2, c * CH, (c + 1) * CH)
+        gather_v(high[1][:, 0, :], 2, CH, 2 * CH)
+
+        gather_v(high[0][:, 1, 0:CH // 2], 3, 0, CH // 2)
+        gather_s(high[0][:, 1, CH // 2:CH], 3, CH // 2, CH)
+        gather_v(high[1][:, 1, :], 3, CH, 2 * CH)
+        gather_s(high[2][:, 1, :], 3, 2 * CH, 3 * CH)
+        gather_s(high[3][:, 1, :], 3, 3 * CH, 4 * CH)
+        nc.vector.tensor_copy(*weave_views(0, 2, high[0][:]))
+        nc.vector.tensor_copy(*weave_views(1, 2, high[1][:]))
+        quant_x(0)
+        nc.scalar.activation(*weave_views(2, 2, high[2][:]), COPY)
+        quant_x(1)
+        nc.scalar.activation(*weave_views(3, 2, high[3][:]), COPY)
+        quant_x(2)
+        quant_x(3)
 
         cols = CH // 16
-
-        def gather(tile, source, c):
-            nc.vector.tensor_copy(tile[:], source[:].indirect(offs_t[:, c * cols:(c + 1) * cols]))
-
-        gw0_t = keep.tile([P, CH], U32, name="gw0", align_bytes=64)
-        gb0_t = keep.tile([P, CH], U8, name="gb0", align_bytes=64)
-        gather(gw0_t, x_words, 0)
-        gather(gb0_t, x_bytes, 0)
-        gw0, gb0 = gw0_t[:], gb0_t[:]
-        for u in range(2):
-            warm = psum.tile([32, PACK * CH], F32, name="warm%d" % u, tag="y%d" % (2 + u))
-            nc.tensor.matmul_mx(out=warm[:], lhsT=gw0[:, 0:32].bitcast(FP8X4), lhsT_scale=warm_bytes[:, 0:32],
-                                rhs=warm_words[:].bitcast(FP8X4), rhs_scale=warm_bytes[:], start=True, stop=True)
-        gw1_t = keep.tile([P, CH], U32, name="gw1", align_bytes=64)
-        gb1_t = keep.tile([P, CH], U8, name="gb1", align_bytes=64)
-        gw1, gb1 = gw1_t[:], gb1_t[:]
-
-        round_w(1)
-        gather(gw1_t, x_words, 1)
-        quant_w(1)
-        gather(gb1_t, x_bytes, 1)
-        round_w(2)
-        round_w(3)
-        gb2 = late.tile([P, CH], U8, name="gb2", offset=THIRD_AT, align_bytes=64)
-        gather(gb2, x_bytes, 2)
-        quant_w(2)
-
-        gw2 = late.tile([P, CH], U32, name="gw2", offset=RAW_AT, align_bytes=64)
-        gw3 = late.tile([P, CH], U32, name="gw3", offset=RAW_AT + 1024, align_bytes=64)
-        gb3 = late.tile([P, CH], U8, name="gb3", offset=RAW_AT + 640, align_bytes=64)
-        g_words = [gw0, gw1, gw2[:], gw3[:]]
-        g_bytes = [gb0, gb1, gb2[:], gb3[:]]
-        h_grouped = [late.tile([P, CH, PACK], BF16, name="h_grouped%d" % c, offset=H0_AT + 1024 * c, align_bytes=64) for c in range(4)]
-        h_words = [late.tile([P, CH], U32, name="h_words%d" % c, offset=Q_AT + [0, 1024, 2048, 3072][c], align_bytes=64) for c in range(4)]
-        h_bytes = [late.tile([P, CH], U8, name="h_bytes%d" % c, offset=Q_AT + [512, 1536, 2560, 3584][c], align_bytes=64) for c in range(4)]
-        groups = [1,3]
+        h_grouped = [keep.tile([P, CH, PACK], BF16, name="h_grouped%d" % c, align_bytes=64) for c in range(4)]
+        h_words = [keep.tile([P, CH], U32, name="h_words%d" % c, align_bytes=64) for c in range(4)]
+        h_bytes = [keep.tile([P, CH], U8, name="h_bytes%d" % c, align_bytes=64) for c in range(4)]
+        groups = [1, 3]
         y_tiles = [keep.tile([P, g * CH], F32, name="y%d" % i) for i, g in enumerate(groups)]
         places = [(i, e) for i, g in enumerate(groups) for e in range(g)]
 
         def first(c, t0, t1, tag):
             acc = psum.tile([P, t1 - t0, CH], F32, name="h_acc%d_%d" % (c, t0), tag=tag)
             for t in range(t0, t1):
-                nc.tensor.matmul_mx(out=acc[:, t - t0, :], lhsT=w_words[t].bitcast(FP8X4), lhsT_scale=w_bytes[t],
-                                    rhs=g_words[c].bitcast(FP8X4), rhs_scale=g_bytes[c], start=True, stop=True)
+                nc.tensor.matmul_mx(out=acc[:, t - t0, :], lhsT=w_words[:, t * P:(t + 1) * P].bitcast(FP8X4), lhsT_scale=w_bytes[:, t * P:(t + 1) * P],
+                                    rhs=g_words[c][:].bitcast(FP8X4), rhs_scale=g_bytes[c][:], start=True, stop=True)
             return acc
 
         def relu_s(c, t0, t1, acc):
@@ -186,17 +151,10 @@ def tile_picked_route2_mlprelu_e_kernel(tc, xT, gate, w1, w2_words, w2_scales, o
             i, e = places[c]
             nc.scalar.activation(y_tiles[i][:, e * CH:(e + 1) * CH], acc[:], COPY)
 
-        def empty_v(c, acc):
-            i, e = places[c]
-            nc.vector.tensor_copy(y_tiles[i][:, e * CH:(e + 1) * CH], acc[:])
-
         def scatter(i):
             a, b = sum(groups[:i]), sum(groups[:i + 1])
             nc.vector.tensor_tensor(window[:].indirect(dst_t[:, a * cols:b * cols]), y_tiles[i][:], gate_t[:, a * CH:b * CH], MULT)
 
-        gather(gw2, x_words, 2)
-        gather(gw3, x_words, 3)
-        gather(gb3, x_bytes, 3)
         relu_s(0, 0, 4, first(0, 0, 4, "a0"))
         relu_v(1, 0, 4, first(1, 0, 4, "b"))
         quant(0)

@@ -22,13 +22,13 @@ PACK = 4
 CH = 128
 W_VECTOR = 88
 WARM_M = 32
+WARM_AT = 320
 
 
 def tile_picked_route2_mlprelu_e_kernel(tc, xT, gate, w1, w2_words, w2_scales, offs, dst, out):
     nc = tc.nc
     with ExitStack() as ctx:
         keep = ctx.enter_context(tc.tile_pool(name="keep", bufs=1))
-        late = ctx.enter_context(tc.tile_pool(name="late", bufs=1))
         psum = ctx.enter_context(tc.psum_pool(name="psum", bufs=1))
 
         offs_t = keep.tile([P, S // 16], U16, name="offs_t")
@@ -41,7 +41,7 @@ def tile_picked_route2_mlprelu_e_kernel(tc, xT, gate, w1, w2_words, w2_scales, o
 
         x_view = xT.rearrange("(p j) t -> p j t", j=PACK)
         w_raw = keep.tile([P, PACK, H], F32, name="w_raw")
-        planes = [late.tile([P, T], F32, name="plane%d" % j, offset=4 * T * j, align_bytes=64) for j in range(PACK)]
+        planes = [keep.tile([P, T], F32, name="plane%d" % j) for j in range(PACK)]
 
         nc.sync.dma_start(w_raw[:], w1.rearrange("(p j) c -> p j c", j=PACK))
         nc.sync.dma_start(offs_t[:], offs)
@@ -65,55 +65,61 @@ def tile_picked_route2_mlprelu_e_kernel(tc, xT, gate, w1, w2_words, w2_scales, o
         nc.scalar.activation(*w_views(W_VECTOR, P), COPY)
         nc.vector.quantize_mx(out=w_words[:].bitcast(FP8X4), scales=w_bytes[:], in_=w_grouped[:].rearrange("p t m j -> p (t m j)"))
 
-        low = keep.tile([P, 2, S], BF16, name="low")
-        high = [keep.tile([P, 2, CH], BF16, name="high%d" % c) for c in range(4)]
-        x_grouped = [keep.tile([P, CH, PACK], BF16, name="x_grouped%d" % c, align_bytes=64) for c in range(4)]
+        picked = [keep.tile([P, 2, S], BF16, name="picked%d" % u, align_bytes=64) for u in range(2)]
+        x_grouped = keep.tile([P, S, PACK], BF16, name="x_grouped", align_bytes=64)
         g_words = [keep.tile([P, CH], U32, name="g_words%d" % c, align_bytes=64) for c in range(4)]
         g_bytes = [keep.tile([P, CH], U8, name="g_bytes%d" % c, align_bytes=64) for c in range(4)]
 
-        def gather_v(target, j, a, b):
-            nc.vector.tensor_copy(target, planes[j][:].indirect(offs_t[:, a // 16:b // 16]))
+        def gather_v(j, a, b):
+            nc.vector.tensor_copy(picked[j // 2][:, j % 2, a:b], planes[j][:].indirect(offs_t[:, a // 16:b // 16]))
 
-        def gather_s(target, j, a, b):
-            nc.scalar.activation(target, planes[j][:].indirect(offs_t[:, a // 16:b // 16]), COPY)
+        def gather_s(j, a, b):
+            nc.scalar.activation(picked[j // 2][:, j % 2, a:b], planes[j][:].indirect(offs_t[:, a // 16:b // 16]), COPY)
 
-        def weave_views(c, t0, source):
-            return (x_grouped[c][:, :, t0:t0 + 2].rearrange("p (n i) t -> p n t i", i=4),
-                    source.rearrange("p t (n i) -> p n t i", i=4))
+        def weave_views(u, a, b):
+            return (x_grouped[:, a:b, 2 * u:2 * u + 2].rearrange("p (n i) t -> p n t i", i=4),
+                    picked[u][:, :, a:b].rearrange("p t (n i) -> p n t i", i=4))
+
+        def weave_v(u, a, b):
+            nc.vector.tensor_copy(*weave_views(u, a, b))
+
+        def weave_s(u, a, b):
+            nc.scalar.activation(*weave_views(u, a, b), COPY)
 
         def quant_x(c):
-            nc.vector.quantize_mx(out=g_words[c][:].bitcast(FP8X4), scales=g_bytes[c][:], in_=x_grouped[c][:].rearrange("p n t -> p (n t)"))
+            nc.vector.quantize_mx(out=g_words[c][:].bitcast(FP8X4), scales=g_bytes[c][:],
+                                  in_=x_grouped[:, c * CH:(c + 1) * CH, :].rearrange("p n t -> p (n t)"))
 
-        gather_s(low[:, 0, :], 0, 0, S)
-        gather_v(low[:, 1, 0:S // 2], 1, 0, S // 2)
-        gather_s(low[:, 1, S // 2:S], 1, S // 2, S)
+        gather_s(0, 0, S)
+        gather_v(1, 0, S // 2)
+        gather_s(1, S // 2, S)
+        weave_v(0, 0, CH)
+        weave_v(0, CH, WARM_AT)
 
-        warm_words = late.tile([P, WARM_M], U32, name="warm_words", offset=4 * T, align_bytes=64)
+        warm_words = keep.tile([P, WARM_M], U32, name="warm_words", align_bytes=64)
         warm_bytes = keep.tile([P, WARM_M], U8, name="warm_bytes", align_bytes=64)
-        nc.vector.quantize_mx(out=warm_words[:].bitcast(FP8X4), scales=warm_bytes[:],
-                              in_=w_grouped[:, 0, 0:WARM_M, :].rearrange("p m j -> p (m j)"))
+        nc.vector.quantize_mx(out=warm_words[:].bitcast(FP8X4), scales=warm_bytes[:], in_=picked[0][:, 1, S - PACK * WARM_M:S])
         for u in range(2):
             warm = psum.tile([WARM_M, H], F32, name="warm%d" % u, tag="y%d" % (2 + u))
             nc.tensor.matmul_mx(out=warm[:], lhsT=warm_words[:].bitcast(FP8X4), lhsT_scale=warm_bytes[:],
                                 rhs=w_words[:].bitcast(FP8X4), rhs_scale=w_bytes[:], start=True, stop=True)
 
-        for c in range(4):
-            nc.vector.tensor_copy(*weave_views(c, 0, low[:, :, c * CH:(c + 1) * CH]))
-        for c in (0, 2, 3):
-            gather_s(high[c][:, 0, :], 2, c * CH, (c + 1) * CH)
-        gather_v(high[1][:, 0, :], 2, CH, 2 * CH)
+        weave_v(0, WARM_AT, S)
+        gather_s(2, 0, CH)
+        gather_s(2, 2 * CH, S)
+        gather_v(2, CH, 2 * CH)
 
-        gather_v(high[0][:, 1, 0:CH // 2], 3, 0, CH // 2)
-        gather_s(high[0][:, 1, CH // 2:CH], 3, CH // 2, CH)
-        gather_v(high[1][:, 1, :], 3, CH, 2 * CH)
-        gather_s(high[2][:, 1, :], 3, 2 * CH, 3 * CH)
-        gather_s(high[3][:, 1, :], 3, 3 * CH, 4 * CH)
-        nc.vector.tensor_copy(*weave_views(0, 2, high[0][:]))
-        nc.vector.tensor_copy(*weave_views(1, 2, high[1][:]))
+        gather_v(3, 0, CH // 2)
+        gather_s(3, CH // 2, CH)
+        gather_v(3, CH, 2 * CH)
+        gather_s(3, 2 * CH, 3 * CH)
+        gather_s(3, 3 * CH, S)
+        weave_v(1, 0, CH)
+        weave_v(1, CH, 2 * CH)
         quant_x(0)
-        nc.scalar.activation(*weave_views(2, 2, high[2][:]), COPY)
+        weave_s(1, 2 * CH, 3 * CH)
         quant_x(1)
-        nc.scalar.activation(*weave_views(3, 2, high[3][:]), COPY)
+        weave_s(1, 3 * CH, S)
         quant_x(2)
         quant_x(3)
 
@@ -171,5 +177,4 @@ def tile_picked_route2_mlprelu_e_kernel(tc, xT, gate, w1, w2_words, w2_scales, o
         empty_s(3, second(3, "y3"))
         scatter(1)
 
-        nc.sync.dma_start(out[:, 0:U // 2], window[:, 0:U // 2])
-        nc.scalar.dma_start(out[:, U // 2:U], window[:, U // 2:U])
+        nc.sync.dma_start(out, window[:])

@@ -22,7 +22,7 @@ PACK = 4
 CH = 128
 W_VECTOR = 88
 WARM_M = 32
-WARM_AT = 320
+WARM_AT = 288
 
 
 def tile_picked_route2_mlprelu_e_kernel(tc, xT, gate, w1, w2_words, w2_scales, offs, dst, out):
@@ -84,7 +84,7 @@ def tile_picked_route2_mlprelu_e_kernel(tc, xT, gate, w1, w2_words, w2_scales, o
             nc.vector.tensor_copy(*weave_views(u, a, b))
 
         def weave_s(u, a, b):
-            nc.scalar.activation(*weave_views(u, a, b), COPY)
+            nc.scalar.copy(*weave_views(u, a, b))
 
         def quant_x(c):
             nc.vector.quantize_mx(out=g_words[c][:].bitcast(FP8X4), scales=g_bytes[c][:],
@@ -155,7 +155,7 @@ def tile_picked_route2_mlprelu_e_kernel(tc, xT, gate, w1, w2_words, w2_scales, o
 
         def empty_s(c, acc):
             i, e = places[c]
-            nc.scalar.activation(y_tiles[i][:, e * CH:(e + 1) * CH], acc[:], COPY)
+            nc.scalar.copy(y_tiles[i][:, e * CH:(e + 1) * CH], acc[:])
 
         def scatter(i):
             a, b = sum(groups[:i]), sum(groups[:i + 1])

from contextlib import ExitStack

import concourse.mybir as mybir

K, T, S, H, N, U = 512, 1024, 512, 512, 128, 1024
FLOPS = 2 * K * H * S + 2 * H * N * S

F32 = mybir.dt.float32
BF16 = mybir.dt.bfloat16
I32 = mybir.dt.int32
U32 = mybir.dt.uint32
U16 = mybir.dt.uint16
U8 = mybir.dt.uint8
FP8X4 = mybir.dt.float8_e4m3fn_x4
FP4X4 = mybir.dt.float4_e2m1fn_x4
COPY = mybir.ActivationFunctionType.Copy
RELU = mybir.ActivationFunctionType.Relu
MULT = mybir.AluOpType.mult

P = 128
PACK = 4
CH = 128
W_VECTOR = 88
WARM_M = 32
WARM_AT = 288


def tile_picked_route2_mlprelu_e_kernel(tc, xT, gate, w1, w2_words, w2_scales, offs, dst, out):
    nc = tc.nc
    with ExitStack() as ctx:
        keep = ctx.enter_context(tc.tile_pool(name="keep", bufs=1))
        psum = ctx.enter_context(tc.psum_pool(name="psum", bufs=1))

        offs_t = keep.tile([P, S // 16], U16, name="offs_t")
        dst_t = keep.tile([P, S // 16], U16, name="dst_t")
        w2_codes = keep.tile([P, 2 * N], U8, name="w2_codes", align_bytes=64)
        w2_plane = keep.tile([P, N], U8, name="w2_plane", align_bytes=64)
        gate_t = keep.tile([P, S], F32, name="gate_t")
        window = keep.tile([P, U], F32, name="window")
        nc.vector.memset(window[:], 0.0)

        x_view = xT.rearrange("(p j) t -> p j t", j=PACK)
        w_raw = keep.tile([P, PACK, H], F32, name="w_raw")
        planes = [keep.tile([P, T], F32, name="plane%d" % j) for j in range(PACK)]

        nc.sync.dma_start(w_raw[:], w1.rearrange("(p j) c -> p j c", j=PACK))
        nc.sync.dma_start(offs_t[:], offs)
        for j in range(PACK):
            nc.sync.dma_start(planes[j][:], x_view[:, j, :])
        nc.sync.dma_start(w2_codes[:].bitcast(I32), w2_words[0].bitcast(I32))
        for q in range(4):
            nc.sync.dma_start(w2_plane[32 * q:32 * q + 4, :].bitcast(I32), w2_scales[0, 4 * q:4 * q + 4, :].bitcast(I32))
        nc.sync.dma_start(dst_t[:], dst)
        nc.sync.dma_start(gate_t[:], gate)

        w_grouped = keep.tile([P, PACK, P, PACK], BF16, name="w_grouped", align_bytes=64)
        w_words = keep.tile([P, H], U32, name="w_words", align_bytes=64)
        w_bytes = keep.tile([P, H], U8, name="w_bytes", align_bytes=64)

        def w_views(a, b):
            return (w_grouped[:, :, a:b, :].rearrange("p t m j -> p m j t"),
                    w_raw[:, :, PACK * a:PACK * b].rearrange("p j (m t) -> p m j t", t=PACK))

        nc.vector.tensor_copy(*w_views(0, W_VECTOR))
        nc.scalar.activation(*w_views(W_VECTOR, P), COPY)
        nc.vector.quantize_mx(out=w_words[:].bitcast(FP8X4), scales=w_bytes[:], in_=w_grouped[:].rearrange("p t m j -> p (t m j)"))

        picked = [keep.tile([P, 2, S], BF16, name="picked%d" % u, align_bytes=64) for u in range(2)]
        x_grouped = keep.tile([P, S, PACK], BF16, name="x_grouped", align_bytes=64)
        g_words = [keep.tile([P, CH], U32, name="g_words%d" % c, align_bytes=64) for c in range(4)]
        g_bytes = [keep.tile([P, CH], U8, name="g_bytes%d" % c, align_bytes=64) for c in range(4)]

        def gather_v(j, a, b):
            nc.vector.tensor_copy(picked[j // 2][:, j % 2, a:b], planes[j][:].indirect(offs_t[:, a // 16:b // 16]))

        def gather_s(j, a, b):
            nc.scalar.activation(picked[j // 2][:, j % 2, a:b], planes[j][:].indirect(offs_t[:, a // 16:b // 16]), COPY)

        def weave_views(u, a, b):
            return (x_grouped[:, a:b, 2 * u:2 * u + 2].rearrange("p (n i) t -> p n t i", i=4),
                    picked[u][:, :, a:b].rearrange("p t (n i) -> p n t i", i=4))

        def weave_v(u, a, b):
            nc.vector.tensor_copy(*weave_views(u, a, b))

        def weave_s(u, a, b):
            nc.scalar.copy(*weave_views(u, a, b))

        def quant_x(c):
            nc.vector.quantize_mx(out=g_words[c][:].bitcast(FP8X4), scales=g_bytes[c][:],
                                  in_=x_grouped[:, c * CH:(c + 1) * CH, :].rearrange("p n t -> p (n t)"))

        gather_s(0, 0, S)
        gather_v(1, 0, S // 2)
        gather_s(1, S // 2, S)
        weave_v(0, 0, CH)
        weave_v(0, CH, WARM_AT)

        warm_words = keep.tile([P, WARM_M], U32, name="warm_words", align_bytes=64)
        warm_bytes = keep.tile([P, WARM_M], U8, name="warm_bytes", align_bytes=64)
        nc.vector.quantize_mx(out=warm_words[:].bitcast(FP8X4), scales=warm_bytes[:], in_=picked[0][:, 1, S - PACK * WARM_M:S])
        for u in range(2):
            warm = psum.tile([WARM_M, H], F32, name="warm%d" % u, tag="y%d" % (2 + u))
            nc.tensor.matmul_mx(out=warm[:], lhsT=warm_words[:].bitcast(FP8X4), lhsT_scale=warm_bytes[:],
                                rhs=w_words[:].bitcast(FP8X4), rhs_scale=w_bytes[:], start=True, stop=True)

        weave_v(0, WARM_AT, S)
        gather_s(2, 0, CH)
        gather_s(2, 2 * CH, S)
        gather_v(2, CH, 2 * CH)

        gather_v(3, 0, CH // 2)
        gather_s(3, CH // 2, CH)
        gather_v(3, CH, 2 * CH)
        gather_s(3, 2 * CH, 3 * CH)
        gather_s(3, 3 * CH, S)
        weave_v(1, 0, CH)
        weave_v(1, CH, 2 * CH)
        quant_x(0)
        weave_s(1, 2 * CH, 3 * CH)
        quant_x(1)
        weave_s(1, 3 * CH, S)
        quant_x(2)
        quant_x(3)

        cols = CH // 16
        h_grouped = [keep.tile([P, CH, PACK], BF16, name="h_grouped%d" % c, align_bytes=64) for c in range(4)]
        h_words = [keep.tile([P, CH], U32, name="h_words%d" % c, align_bytes=64) for c in range(4)]
        h_bytes = [keep.tile([P, CH], U8, name="h_bytes%d" % c, align_bytes=64) for c in range(4)]
        groups = [1, 3]
        y_tiles = [keep.tile([P, g * CH], F32, name="y%d" % i) for i, g in enumerate(groups)]
        places = [(i, e) for i, g in enumerate(groups) for e in range(g)]

        def first(c, t0, t1, tag):
            acc = psum.tile([P, t1 - t0, CH], F32, name="h_acc%d_%d" % (c, t0), tag=tag)
            for t in range(t0, t1):
                nc.tensor.matmul_mx(out=acc[:, t - t0, :], lhsT=w_words[:, t * P:(t + 1) * P].bitcast(FP8X4), lhsT_scale=w_bytes[:, t * P:(t + 1) * P],
                                    rhs=g_words[c][:].bitcast(FP8X4), rhs_scale=g_bytes[c][:], start=True, stop=True)
            return acc

        def relu_s(c, t0, t1, acc):
            nc.scalar.activation(h_grouped[c][:, :, t0:t1], acc[:].rearrange("p t n -> p n t"), RELU)

        def relu_v(c, t0, t1, acc):
            nc.vector.tensor_scalar_max(h_grouped[c][:, :, t0:t1], acc[:].rearrange("p t n -> p n t"), 0.0)

        def quant(c):
            nc.vector.quantize_mx(out=h_words[c][:].bitcast(FP8X4), scales=h_bytes[c][:], in_=h_grouped[c][:].rearrange("p n t -> p (n t)"))

        def second(c, tag):
            acc = psum.tile([P, CH], F32, name="y_acc%d" % c, tag=tag)
            nc.tensor.matmul_mx(out=acc[:], lhsT=w2_codes[:].bitcast(FP4X4), lhsT_scale=w2_plane[:],
                                rhs=h_words[c][:].bitcast(FP8X4), rhs_scale=h_bytes[c][:], start=True, stop=True)
            return acc

        def empty_s(c, acc):
            i, e = places[c]
            nc.scalar.copy(y_tiles[i][:, e * CH:(e + 1) * CH], acc[:])

        def scatter(i):
            a, b = sum(groups[:i]), sum(groups[:i + 1])
            nc.vector.tensor_tensor(window[:].indirect(dst_t[:, a * cols:b * cols]), y_tiles[i][:], gate_t[:, a * CH:b * CH], MULT)

        relu_s(0, 0, 4, first(0, 0, 4, "a0"))
        relu_v(1, 0, 4, first(1, 0, 4, "b"))
        quant(0)
        relu_s(2, 0, 4, first(2, 0, 4, "c0"))
        quant(1)
        relu_v(3, 0, 2, first(3, 0, 2, "a1"))
        relu_s(3, 2, 4, first(3, 2, 4, "y3"))
        empty_s(0, second(0, "y0"))
        quant(2)
        quant(3)
        scatter(0)
        empty_s(1, second(1, "y1"))
        empty_s(2, second(2, "y2"))
        empty_s(3, second(3, "y3"))
        scatter(1)

        nc.sync.dma_start(out, window[:])
